import numpy as np
import ml_dtypes


def mxq(x, axis, fmt="e4m3"):
    dtype, down = {"e4m3": (ml_dtypes.float8_e4m3fn, 7), "e5m2": (ml_dtypes.float8_e5m2, 14)}[fmt]
    v = np.moveaxis(np.asarray(x, np.float32).astype(ml_dtypes.bfloat16).astype(np.float64), axis, -1)
    blocks = v.reshape(v.shape[:-1] + (-1, 32))
    amax = np.abs(blocks).max(-1, keepdims=True)
    byte = np.maximum(np.where(amax > 0, np.frexp(amax)[1] - 1 + 127, 0) - down, 1)
    scale = np.exp2(byte - 127.0)
    codes = (blocks / scale).astype(np.float32).astype(dtype).astype(np.float64)
    return np.moveaxis((codes * scale).reshape(v.shape), -1, axis)


WIDE = False


def mx_kscale(k):
    if not WIDE:
        return np.ones(k)
    levels = np.array([10, -10, 5, -5, 0])
    if k % 512:
        return np.exp2(np.random.permutation(np.resize(levels, k // 32))).repeat(32)
    a = np.empty((k // 512, 16))
    for p in range(k // 512):
        a[p, :8] = np.random.permutation(np.resize(levels, 8))
        for g in range(8):
            far = levels[np.abs(levels - a[p, g]) >= 10]
            a[p, g + 8] = far[np.random.randint(len(far))]
    return np.exp2(a.ravel()).repeat(32)


def f64(x):
    return np.asarray(x).astype(np.float64)


def striped(idx):
    return np.tile(idx.reshape(-1, 16).T, (8, 1)).astype(np.uint16)


def unstriped(offs):
    return offs[:16].T.reshape(-1).astype(np.int64)


def pack_weight(w):
    k, n = w.shape
    w = f64(np.asarray(w, np.float32).astype(ml_dtypes.bfloat16)).reshape(k // 32, 32, n)
    amax = np.abs(w).max(1)
    byte = np.clip(np.where(amax > 0, np.frexp(amax)[1] - 1 + 127 - 7, 1), 1, 254)
    scaled = (w * np.exp2(127.0 - byte)[:, None, :]).reshape(k, n).astype(np.float32)
    words = np.ascontiguousarray(scaled.reshape(k // 512, 128, 4, n).transpose(0, 1, 3, 2)).astype(ml_dtypes.float8_e4m3fn).view(np.uint8)
    return words, np.ascontiguousarray(byte.astype(np.uint8).reshape(k // 512, 16, n))


def unpack_weight(words, scales):
    g, p, n, _ = words.shape
    vals = np.ascontiguousarray(words).view(ml_dtypes.float8_e4m3fn).astype(np.float64) * np.repeat(np.exp2(scales.astype(np.float64) - 127.0), 8, axis=1)[..., None]
    return vals.transpose(0, 1, 3, 2).reshape(g * 512, n)


def silu(v):
    return v / (1.0 + np.exp(-np.maximum(v, -700.0)))


K, T, S, W, V, H, G = 512, 2048, 512, 1024, 512, 512, 2048


def setup_inputs():
    n = np.random.standard_normal
    s = mx_kscale(K)[:, None]
    u = mx_kscale(H)
    packed_xT = pack_weight(n((K, T)) * s)
    packed_eT = pack_weight(n((K, W)) * s)
    packed_vT = pack_weight(n((H, G)) / np.sqrt(H) / u[:, None])
    return {
        "x_words": packed_xT[0],
        "x_scales": packed_xT[1],
        "e_words": packed_eT[0],
        "e_scales": packed_eT[1],
        "w1": (n((K, H)) / np.sqrt(2 * K) / s * u).astype(np.float32),
        "w2": (n((K, H)) / np.sqrt(2 * K) / s * u).astype(np.float32),
        "v_words": packed_vT[0],
        "v_scales": packed_vT[1],
        "offs": striped(np.random.permutation(T)[:S]),
        "tok": striped(np.random.permutation(W)[:S]),
        "cand": striped(np.random.permutation(G)[:V]),
    }


def reference(x_words, x_scales, e_words, e_scales, w1, w2, v_words, v_scales, offs, tok, cand):
    xq = unpack_weight(x_words, x_scales)[:, unstriped(offs)]
    e_tok = unpack_weight(e_words, e_scales)[:, unstriped(tok)]
    h = silu(mxq(f64(w1), 0, "e4m3").T @ xq + mxq(f64(w2), 0, "e4m3").T @ e_tok)
    v_cand = unpack_weight(v_words, v_scales)[:, unstriped(cand)]
    y = mxq(h, 0, "e4m3").T @ v_cand
    e = np.exp(y - y.max(axis=1, keepdims=True))
    return e / e.sum(axis=1, keepdims=True)

@@ -1,0 +1,178 @@
+from contextlib import ExitStack
+
+import concourse.mybir as mybir
+
+K, T, S, W, V, H, G = 512, 2048, 512, 1024, 512, 512, 2048
+FLOPS = 2 * (2 * K * H * S + H * S * V)
+
+F32 = mybir.dt.float32
+BF16 = mybir.dt.bfloat16
+I32 = mybir.dt.int32
+U32 = mybir.dt.uint32
+U16 = mybir.dt.uint16
+U8 = mybir.dt.uint8
+FP8X4 = mybir.dt.float8_e4m3fn_x4
+ACT = mybir.ActivationFunctionType
+ALU = mybir.AluOpType
+AX = mybir.AxisListType
+
+P = 128
+PACK = 4
+NODE_TILE = 128
+X_ROW, E_ROW, V_ROW = 0, 4, 8
+W2_VECTOR_SHARE = 88
+
+
+def tile_picked_zfrs_silu_p_kernel(
+    tc, x_words, x_scales, e_words, e_scales, w1, w2, v_words, v_scales, offs, tok, cand, out
+):
+    nc = tc.nc
+    with ExitStack() as ctx:
+        keep = ctx.enter_context(tc.tile_pool(name="keep", bufs=1))
+        psum = ctx.enter_context(tc.psum_pool(name="psum", bufs=1))
+
+        def load_list(name, src):
+            t = keep.tile([P, S // 16], U16, name=name)
+            nc.sync.dma_start(t[:], src)
+            return t
+
+        def load_scales(name, src, width, row, queues, clear, tag):
+            t = keep.tile([P, width], U8, name=name, tag=tag, align_bytes=64)
+            clear.memset(t[:].bitcast(I32), 0)
+            for q in range(4):
+                queues[q].dma_start(
+                    t[32 * q + row : 32 * q + row + 4, :].bitcast(I32),
+                    src[0, 4 * q : 4 * q + 4, :].bitcast(I32),
+                )
+            return t
+
+        def load_words(name, src, width, tag):
+            t = keep.tile([P, width], I32, name=name, tag=tag, align_bytes=64)
+            nc.sync.dma_start(t[:], src[0].rearrange("p n t -> p (n t)").bitcast(I32))
+            return t
+
+        def load_weight(name, src):
+            t = keep.tile([P, PACK, H], F32, name=name, tag=name, align_bytes=64)
+            nc.sync.dma_start(t[:], src.rearrange("(p r) c -> p r c", r=PACK))
+            return t
+
+        offs_t = load_list("offs_t", offs)
+        tok_t = load_list("tok_t", tok)
+        cand_t = load_list("cand_t", cand)
+        w1_raw = load_weight("w1_raw", w1)
+        w2_raw = load_weight("w2_raw", w2)
+        xs_tab = load_scales("xs_tab", x_scales, T, X_ROW, [nc.scalar] * 4, nc.vector, "x_tab")
+        es_tab = load_scales(
+            "es_tab", e_scales, W, E_ROW, [nc.scalar] * 2 + [nc.gpsimd] * 2, nc.vector, "e_tab"
+        )
+        vs_tab = load_scales("vs_tab", v_scales, G, V_ROW, [nc.gpsimd] * 4, nc.gpsimd, "vs_tab")
+
+        def gather_scales(name, tab, lst):
+            t = keep.tile([P, S], U8, name=name, align_bytes=64)
+            nc.vector.tensor_copy(t[:], tab[:].indirect(lst[:]))
+            return t
+
+        def gather_words(dst, tab, lst, lo, hi):
+            nc.vector.tensor_copy(
+                dst[:, lo:hi], tab[:].bitcast(U32).indirect(lst[:, lo // 16 : hi // 16])
+            )
+
+        xs = gather_scales("xs", xs_tab, offs_t)
+        xw_tab = load_words("xw_tab", x_words, T, "x_tab")
+        es = gather_scales("es", es_tab, tok_t)
+        ew_tab = load_words("ew_tab", e_words, W, "e_tab")
+        vs = gather_scales("vs", vs_tab, cand_t)
+
+        def grouped_views(raw, grouped, lo, hi):
+            dst = grouped[:].rearrange("p (j m r) -> p m j r", j=PACK, r=PACK)[:, lo:hi]
+            src = raw[:].rearrange("p r (m j) -> p m j r", j=PACK)[:, lo:hi]
+            return dst, src
+
+        w1_bf = keep.tile([P, H * PACK], BF16, name="w1_bf", align_bytes=64)
+        w2_bf = keep.tile([P, H * PACK], BF16, name="w2_bf", align_bytes=64)
+        nc.scalar.copy(*grouped_views(w1_raw, w1_bf, 0, P))
+        vw_tab = load_words("vw_tab", v_words, G, "w1_raw")
+        nc.vector.tensor_copy(*grouped_views(w2_raw, w2_bf, 0, W2_VECTOR_SHARE))
+        nc.scalar.copy(*grouped_views(w2_raw, w2_bf, W2_VECTOR_SHARE, P))
+
+        def quantize(name, src, width):
+            codes = keep.tile([P, width], U32, name=name + "_codes", align_bytes=64)
+            scales = keep.tile([P, width], U8, name=name + "_scales", align_bytes=64)
+            nc.vector.quantize_mx(out=codes[:].bitcast(FP8X4), scales=scales[:], in_=src)
+            return codes, scales
+
+        w1_codes, w1_scales = quantize("w1", w1_bf[:], H)
+        w2_codes, w2_scales = quantize("w2", w2_bf[:], H)
+
+        xw = keep.tile([P, S], U32, name="xw", align_bytes=64)
+        ew = keep.tile([P, S], U32, name="ew", align_bytes=64)
+        vw = keep.tile([P, V], U32, name="vw", align_bytes=64)
+        gather_words(xw, xw_tab, offs_t, 0, 256)
+        gather_words(ew, ew_tab, tok_t, 0, 128)
+        gather_words(ew, ew_tab, tok_t, 128, 256)
+        gather_words(xw, xw_tab, offs_t, 256, 512)
+        gather_words(ew, ew_tab, tok_t, 256, 512)
+
+        tiles = range(S // NODE_TILE)
+        h_bf = []
+        for b in tiles:
+            nodes = slice(b * NODE_TILE, (b + 1) * NODE_TILE)
+            pre = psum.tile([P, PACK, NODE_TILE], F32, name="pre%d" % b)
+            for j in range(PACK):
+                cols = slice(j * P, (j + 1) * P)
+                nc.tensor.matmul_mx(
+                    out=pre[:, j, :],
+                    lhsT=w1_codes[:, cols].bitcast(FP8X4),
+                    lhsT_scale=w1_scales[:, cols],
+                    rhs=xw[:, nodes].bitcast(FP8X4),
+                    rhs_scale=xs[X_ROW:P, nodes],
+                    start=True,
+                    stop=False,
+                )
+                nc.tensor.matmul_mx(
+                    out=pre[:, j, :],
+                    lhsT=w2_codes[:, cols].bitcast(FP8X4),
+                    lhsT_scale=w2_scales[:, cols],
+                    rhs=ew[:, nodes].bitcast(FP8X4),
+                    rhs_scale=es[E_ROW:P, nodes],
+                    start=False,
+                    stop=True,
+                )
+            hb = keep.tile([P, NODE_TILE, PACK], BF16, name="h_bf%d" % b, align_bytes=64)
+            nc.scalar.activation(hb[:], pre[:].rearrange("p j n -> p n j"), ACT.Silu)
+            h_bf.append(hb)
+
+        gather_words(vw, vw_tab, cand_t, 0, V)
+
+        logits = []
+        neg_max = []
+        for b in tiles:
+            h_codes, h_scales = quantize(
+                "h%d" % b, h_bf[b][:].rearrange("p n j -> p (n j)"), NODE_TILE
+            )
+            y = psum.tile([P, V], F32, name="y%d" % b)
+            nc.tensor.matmul_mx(
+                out=y[:],
+                lhsT=h_codes[:].bitcast(FP8X4),
+                lhsT_scale=h_scales[:],
+                rhs=vw[:].bitcast(FP8X4),
+                rhs_scale=vs[V_ROW:P, :],
+                start=True,
+                stop=True,
+            )
+            logits.append(y)
+        for b in tiles:
+            m = keep.tile([P, 1], F32, name="neg_max%d" % b)
+            nc.vector.tensor_reduce(m[:], logits[b][:], AX.X, ALU.max, negate=True)
+            neg_max.append(m)
+        for b in tiles:
+            ex = keep.tile([P, V], F32, name="ex%d" % b)
+            total = keep.tile([P, 1], F32, name="total%d" % b)
+            nc.scalar.activation(
+                ex[:], logits[b][:], ACT.Exp, bias=neg_max[b][:], accum_out=total[:]
+            )
+            inv = keep.tile([P, 1], F32, name="inv%d" % b)
+            nc.vector.reciprocal(inv[:], total[:])
+            res = keep.tile([P, V], F32, name="res%d" % b)
+            nc.vector.tensor_scalar(res[:], ex[:], inv[:], None, ALU.mult)
+            nc.sync.dma_start(out[b * NODE_TILE : (b + 1) * NODE_TILE, :], res[:])

@@ -18,9 +18,12 @@ AX = mybir.AxisListType
 
 P = 128
 PACK = 4
+QUADRANT = 32
+LIST_ROWS = 16
 NODE_TILE = 128
+PRE_BANKS = 2
+WARM_PASSES = 3
 X_ROW, E_ROW, V_ROW = 0, 4, 8
-W2_VECTOR_SHARE = 88
 
 
 def tile_picked_zfrs_silu_p_kernel(
@@ -32,99 +35,117 @@ def tile_picked_zfrs_silu_p_kernel(
         psum = ctx.enter_context(tc.psum_pool(name="psum", bufs=1))
 
         def load_list(name, src):
-            t = keep.tile([P, S // 16], U16, name=name)
-            nc.sync.dma_start(t[:], src)
-            return t
+            lst = keep.tile([P, S // LIST_ROWS], U16, name=name)
+            nc.sync.dma_start(lst[:], src)
+            return lst
 
-        def load_scales(name, src, width, row, queues, clear, tag):
-            t = keep.tile([P, width], U8, name=name, tag=tag, align_bytes=64)
-            clear.memset(t[:].bitcast(I32), 0)
-            for q in range(4):
+        def load_scales(name, src, width, row, queues, tag):
+            table = keep.tile([P, width], U8, name=name, tag=tag, align_bytes=64)
+            nc.vector.memset(table[:].bitcast(I32), 0)
+            for q in range(P // QUADRANT):
+                first = QUADRANT * q + row
                 queues[q].dma_start(
-                    t[32 * q + row : 32 * q + row + 4, :].bitcast(I32),
+                    table[first : first + 4, :].bitcast(I32),
                     src[0, 4 * q : 4 * q + 4, :].bitcast(I32),
                 )
-            return t
+            return table
 
         def load_words(name, src, width, tag):
-            t = keep.tile([P, width], I32, name=name, tag=tag, align_bytes=64)
-            nc.sync.dma_start(t[:], src[0].rearrange("p n t -> p (n t)").bitcast(I32))
-            return t
+            table = keep.tile([P, width], I32, name=name, tag=tag, align_bytes=64)
+            nc.sync.dma_start(table[:], src[0].rearrange("p n r -> p (n r)").bitcast(I32))
+            return table
 
         def load_weight(name, src):
-            t = keep.tile([P, PACK, H], F32, name=name, tag=name, align_bytes=64)
-            nc.sync.dma_start(t[:], src.rearrange("(p r) c -> p r c", r=PACK))
-            return t
+            raw = keep.tile([P, PACK, H], F32, name=name, tag=name, align_bytes=64)
+            nc.sync.dma_start(raw[:], src.rearrange("(p r) c -> p r c", r=PACK))
+            return raw
 
         offs_t = load_list("offs_t", offs)
         tok_t = load_list("tok_t", tok)
         cand_t = load_list("cand_t", cand)
         w1_raw = load_weight("w1_raw", w1)
-        w2_raw = load_weight("w2_raw", w2)
-        xs_tab = load_scales("xs_tab", x_scales, T, X_ROW, [nc.scalar] * 4, nc.vector, "x_tab")
+        warm_in = keep.tile([P, 1], F32, name="warm_in", tag="w2_raw", align_bytes=64)
+        warm_out = keep.tile([P, 1], F32, name="warm_out", tag="slot_vs", align_bytes=64)
+        warm_sum = keep.tile([P, 1], F32, name="warm_sum", tag="slot_x", align_bytes=64)
+        xs_tab = load_scales("xs_tab", x_scales, T, X_ROW, [nc.sync] * 4, "xs_tab")
         es_tab = load_scales(
-            "es_tab", e_scales, W, E_ROW, [nc.scalar] * 2 + [nc.gpsimd] * 2, nc.vector, "e_tab"
+            "es_tab", e_scales, W, E_ROW, [nc.sync] * 2 + [nc.gpsimd] * 2, "es_tab"
         )
-        vs_tab = load_scales("vs_tab", v_scales, G, V_ROW, [nc.gpsimd] * 4, nc.gpsimd, "vs_tab")
 
-        def gather_scales(name, tab, lst):
-            t = keep.tile([P, S], U8, name=name, align_bytes=64)
-            nc.vector.tensor_copy(t[:], tab[:].indirect(lst[:]))
-            return t
+        nc.vector.memset(warm_in[:], 0.0)
+        nc.scalar.activation(warm_out[:], warm_in[:], ACT.Silu, accum_out=warm_sum[:])
+        w2_raw = load_weight("w2_raw", w2)
+        xw_tab = load_words("xw_tab", x_words, T, "slot_x")
+        vs_tab = load_scales("vs_tab", v_scales, G, V_ROW, [nc.sync] * 4, "slot_vs")
 
-        def gather_words(dst, tab, lst, lo, hi):
-            nc.vector.tensor_copy(
-                dst[:, lo:hi], tab[:].bitcast(U32).indirect(lst[:, lo // 16 : hi // 16])
-            )
+        def gather_scales(name, table, lst, tag):
+            picked = keep.tile([P, S], U8, name=name, tag=tag, align_bytes=64)
+            nc.vector.tensor_copy(picked[:], table[:].indirect(lst[:]))
+            return picked
 
-        xs = gather_scales("xs", xs_tab, offs_t)
-        xw_tab = load_words("xw_tab", x_words, T, "x_tab")
-        es = gather_scales("es", es_tab, tok_t)
-        ew_tab = load_words("ew_tab", e_words, W, "e_tab")
-        vs = gather_scales("vs", vs_tab, cand_t)
+        def gather_words(name, table, lst, lo, hi, tag):
+            picked = keep.tile([P, hi - lo], U32, name=name, tag=tag, align_bytes=64)
+            entries = lst[:, lo // LIST_ROWS : hi // LIST_ROWS]
+            nc.vector.tensor_copy(picked[:], table[:].bitcast(U32).indirect(entries))
+            return picked
 
-        def grouped_views(raw, grouped, lo, hi):
-            dst = grouped[:].rearrange("p (j m r) -> p m j r", j=PACK, r=PACK)[:, lo:hi]
-            src = raw[:].rearrange("p r (m j) -> p m j r", j=PACK)[:, lo:hi]
+        xs = gather_scales("xs", xs_tab, offs_t, "xs")
+        es = gather_scales("es", es_tab, tok_t, "xs_tab")
+
+        def grouped_views(raw, grouped):
+            dst = grouped[:].rearrange("p (j m r) -> p m j r", j=PACK, r=PACK)
+            src = raw[:].rearrange("p r (m j) -> p m j r", j=PACK)
             return dst, src
 
         w1_bf = keep.tile([P, H * PACK], BF16, name="w1_bf", align_bytes=64)
         w2_bf = keep.tile([P, H * PACK], BF16, name="w2_bf", align_bytes=64)
-        nc.scalar.copy(*grouped_views(w1_raw, w1_bf, 0, P))
-        vw_tab = load_words("vw_tab", v_words, G, "w1_raw")
-        nc.vector.tensor_copy(*grouped_views(w2_raw, w2_bf, 0, W2_VECTOR_SHARE))
-        nc.scalar.copy(*grouped_views(w2_raw, w2_bf, W2_VECTOR_SHARE, P))
+        nc.scalar.copy(*grouped_views(w1_raw, w1_bf))
+        ew_tab = load_words("ew_tab", e_words, W, "w1_raw")
+        nc.scalar.copy(*grouped_views(w2_raw, w2_bf))
 
-        def quantize(name, src, width):
+        def quantize(name, src, width, scales_tag):
             codes = keep.tile([P, width], U32, name=name + "_codes", align_bytes=64)
-            scales = keep.tile([P, width], U8, name=name + "_scales", align_bytes=64)
+            scales = keep.tile([P, width], U8, name=name + "_scales", tag=scales_tag, align_bytes=64)
             nc.vector.quantize_mx(out=codes[:].bitcast(FP8X4), scales=scales[:], in_=src)
             return codes, scales
 
-        w1_codes, w1_scales = quantize("w1", w1_bf[:], H)
-        w2_codes, w2_scales = quantize("w2", w2_bf[:], H)
+        w1_codes, w1_scales = quantize("w1", w1_bf[:], H, "es_tab")
+        vw_tab = load_words("vw_tab", v_words, G, "w1_bf")
+        w2_codes, w2_scales = quantize("w2", w2_bf[:], H, "w2_scales")
 
-        xw = keep.tile([P, S], U32, name="xw", align_bytes=64)
-        ew = keep.tile([P, S], U32, name="ew", align_bytes=64)
-        vw = keep.tile([P, V], U32, name="vw", align_bytes=64)
-        gather_words(xw, xw_tab, offs_t, 0, 256)
-        gather_words(ew, ew_tab, tok_t, 0, 128)
-        gather_words(ew, ew_tab, tok_t, 128, 256)
-        gather_words(xw, xw_tab, offs_t, 256, 512)
-        gather_words(ew, ew_tab, tok_t, 256, 512)
+        for b in range(WARM_PASSES):
+            idle = psum.tile([P, V], F32, name="idle", tag="y%d" % b)
+            nc.tensor.matmul_mx(
+                out=idle[:],
+                lhsT=w1_codes[:, 0:P].bitcast(FP8X4),
+                lhsT_scale=w1_scales[:, 0:P],
+                rhs=w2_codes[:].bitcast(FP8X4),
+                rhs_scale=w2_scales[:],
+                start=True,
+                stop=True,
+            )
+
+        one, two = NODE_TILE, 2 * NODE_TILE
+        x_first = gather_words("x_first", xw_tab, offs_t, 0, two, "x_first")
+        e_first = gather_words("e_first", ew_tab, tok_t, 0, one, "e_first")
+        e_second = gather_words("e_second", ew_tab, tok_t, one, two, "e_second")
+        x_last = gather_words("x_last", xw_tab, offs_t, two, S, "x_last")
+        e_last = gather_words("e_last", ew_tab, tok_t, two, S, "e_last")
+        xw = [x_first[:, 0:one], x_first[:, one:two], x_last[:, 0:one], x_last[:, one:two]]
+        ew = [e_first[:], e_second[:], e_last[:, 0:one], e_last[:, one:two]]
 
         tiles = range(S // NODE_TILE)
         h_bf = []
         for b in tiles:
             nodes = slice(b * NODE_TILE, (b + 1) * NODE_TILE)
-            pre = psum.tile([P, PACK, NODE_TILE], F32, name="pre%d" % b)
+            pre = psum.tile([P, PACK, NODE_TILE], F32, name="pre", tag="pre%d" % (b % PRE_BANKS))
             for j in range(PACK):
                 cols = slice(j * P, (j + 1) * P)
                 nc.tensor.matmul_mx(
                     out=pre[:, j, :],
                     lhsT=w1_codes[:, cols].bitcast(FP8X4),
                     lhsT_scale=w1_scales[:, cols],
-                    rhs=xw[:, nodes].bitcast(FP8X4),
+                    rhs=xw[b].bitcast(FP8X4),
                     rhs_scale=xs[X_ROW:P, nodes],
                     start=True,
                     stop=False,
@@ -133,7 +154,7 @@ def tile_picked_zfrs_silu_p_kernel(
                     out=pre[:, j, :],
                     lhsT=w2_codes[:, cols].bitcast(FP8X4),
                     lhsT_scale=w2_scales[:, cols],
-                    rhs=ew[:, nodes].bitcast(FP8X4),
+                    rhs=ew[b].bitcast(FP8X4),
                     rhs_scale=es[E_ROW:P, nodes],
                     start=False,
                     stop=True,
@@ -142,13 +163,13 @@ def tile_picked_zfrs_silu_p_kernel(
             nc.scalar.activation(hb[:], pre[:].rearrange("p j n -> p n j"), ACT.Silu)
             h_bf.append(hb)
 
-        gather_words(vw, vw_tab, cand_t, 0, V)
+        vs = gather_scales("vs", vs_tab, cand_t, "w1_raw")
+        vw = gather_words("vw", vw_tab, cand_t, 0, V, "slot_vs")
 
         logits = []
-        neg_max = []
         for b in tiles:
             h_codes, h_scales = quantize(
-                "h%d" % b, h_bf[b][:].rearrange("p n j -> p (n j)"), NODE_TILE
+                "h%d" % b, h_bf[b][:].rearrange("p n j -> p (n j)"), NODE_TILE, "h%d_scales" % b
             )
             y = psum.tile([P, V], F32, name="y%d" % b)
             nc.tensor.matmul_mx(
@@ -161,10 +182,12 @@ def tile_picked_zfrs_silu_p_kernel(
                 stop=True,
             )
             logits.append(y)
+
+        neg_max = []
         for b in tiles:
-            m = keep.tile([P, 1], F32, name="neg_max%d" % b)
-            nc.vector.tensor_reduce(m[:], logits[b][:], AX.X, ALU.max, negate=True)
-            neg_max.append(m)
+            lowest = keep.tile([P, 1], F32, name="neg_max%d" % b)
+            nc.vector.tensor_reduce(lowest[:], logits[b][:], AX.X, ALU.max, negate=True)
+            neg_max.append(lowest)
         for b in tiles:
             ex = keep.tile([P, V], F32, name="ex%d" % b)
             total = keep.tile([P, 1], F32, name="total%d" % b)

@@ -21,7 +21,6 @@ PACK = 4
 QUADRANT = 32
 LIST_ROWS = 16
 NODE_TILE = 128
-PRE_BANKS = 2
 WARM_PASSES = 3
 X_ROW, E_ROW, V_ROW = 0, 4, 8
 
@@ -32,6 +31,7 @@ def tile_picked_zfrs_silu_p_kernel(
     nc = tc.nc
     with ExitStack() as ctx:
         keep = ctx.enter_context(tc.tile_pool(name="keep", bufs=1))
+        lap = ctx.enter_context(tc.tile_pool(name="lap", bufs=1))
         psum = ctx.enter_context(tc.psum_pool(name="psum", bufs=1))
 
         def load_list(name, src):
@@ -39,19 +39,18 @@ def tile_picked_zfrs_silu_p_kernel(
             nc.sync.dma_start(lst[:], src)
             return lst
 
-        def load_scales(name, src, width, row, queues, tag):
-            table = keep.tile([P, width], U8, name=name, tag=tag, align_bytes=64)
+        def clear_scales(table):
             nc.vector.memset(table[:].bitcast(I32), 0)
-            for q in range(P // QUADRANT):
-                first = QUADRANT * q + row
-                queues[q].dma_start(
-                    table[first : first + 4, :].bitcast(I32),
-                    src[0, 4 * q : 4 * q + 4, :].bitcast(I32),
-                )
             return table
 
-        def load_words(name, src, width, tag):
-            table = keep.tile([P, width], I32, name=name, tag=tag, align_bytes=64)
+        def load_scales(table, src, row, queue, rows):
+            for r in rows:
+                queue.dma_start(
+                    table[row + r : P : QUADRANT, :].bitcast(I32),
+                    src[0, r : 16 : PACK, :].bitcast(I32),
+                )
+
+        def load_words(table, src):
             nc.sync.dma_start(table[:], src[0].rearrange("p n r -> p (n r)").bitcast(I32))
             return table
 
@@ -64,54 +63,59 @@ def tile_picked_zfrs_silu_p_kernel(
         tok_t = load_list("tok_t", tok)
         cand_t = load_list("cand_t", cand)
         w1_raw = load_weight("w1_raw", w1)
-        warm_in = keep.tile([P, 1], F32, name="warm_in", tag="w2_raw", align_bytes=64)
-        warm_out = keep.tile([P, 1], F32, name="warm_out", tag="slot_vs", align_bytes=64)
-        warm_sum = keep.tile([P, 1], F32, name="warm_sum", tag="slot_x", align_bytes=64)
-        xs_tab = load_scales("xs_tab", x_scales, T, X_ROW, [nc.sync] * 4, "xs_tab")
-        es_tab = load_scales(
-            "es_tab", e_scales, W, E_ROW, [nc.sync] * 2 + [nc.gpsimd] * 2, "es_tab"
-        )
-
-        nc.vector.memset(warm_in[:], 0.0)
-        nc.scalar.activation(warm_out[:], warm_in[:], ACT.Silu, accum_out=warm_sum[:])
         w2_raw = load_weight("w2_raw", w2)
-        xw_tab = load_words("xw_tab", x_words, T, "slot_x")
-        vs_tab = load_scales("vs_tab", v_scales, G, V_ROW, [nc.sync] * 4, "slot_vs")
 
-        def gather_scales(name, table, lst, tag):
-            picked = keep.tile([P, S], U8, name=name, tag=tag, align_bytes=64)
+        xs_tab = clear_scales(lap.tile([P, T], U8, name="xs_tab", align_bytes=64, offset=0))
+        warm_in = keep.tile([P, 1], F32, name="warm_in", tag="slot_x", align_bytes=64)
+        warm_out = keep.tile([P, 1], F32, name="warm_out", tag="slot_e", align_bytes=64)
+        nc.vector.memset(warm_in[:], 0.0)
+        es_tab = clear_scales(keep.tile([P, W], U8, name="es_tab", tag="es_tab", align_bytes=64))
+        vs_tab = clear_scales(keep.tile([P, G], U8, name="vs_tab", align_bytes=64))
+        load_scales(xs_tab, x_scales, X_ROW, nc.scalar, (0, 1, 2))
+        load_scales(xs_tab, x_scales, X_ROW, nc.gpsimd, (3,))
+        nc.scalar.activation(warm_out[:], warm_in[:], ACT.Silu)
+        load_scales(es_tab, e_scales, E_ROW, nc.scalar, (0, 1))
+        xw_tab = load_words(keep.tile([P, T], I32, name="xw_tab", tag="slot_x", align_bytes=64), x_words)
+        ew_tab = load_words(keep.tile([P, W], I32, name="ew_tab", tag="slot_e", align_bytes=64), e_words)
+        load_scales(es_tab, e_scales, E_ROW, nc.gpsimd, (2, 3))
+        load_scales(vs_tab, v_scales, V_ROW, nc.gpsimd, range(PACK))
+
+        def gather_scales(picked, table, lst):
             nc.vector.tensor_copy(picked[:], table[:].indirect(lst[:]))
             return picked
 
-        def gather_words(name, table, lst, lo, hi, tag):
-            picked = keep.tile([P, hi - lo], U32, name=name, tag=tag, align_bytes=64)
+        def gather_words(name, table, lst, lo, hi, tag=None):
+            picked = keep.tile([P, hi - lo], U32, name=name, tag=tag or name, align_bytes=64)
             entries = lst[:, lo // LIST_ROWS : hi // LIST_ROWS]
             nc.vector.tensor_copy(picked[:], table[:].bitcast(U32).indirect(entries))
             return picked
 
-        xs = gather_scales("xs", xs_tab, offs_t, "xs")
-        es = gather_scales("es", es_tab, tok_t, "xs_tab")
+        xs = gather_scales(keep.tile([P, S], U8, name="xs", align_bytes=64), xs_tab, offs_t)
+        es = gather_scales(lap.tile([P, S], U8, name="es", align_bytes=64, offset=0), es_tab, tok_t)
 
-        def grouped_views(raw, grouped):
+        def grouped_views(raw, grouped, lo, hi):
             dst = grouped[:].rearrange("p (j m r) -> p m j r", j=PACK, r=PACK)
             src = raw[:].rearrange("p r (m j) -> p m j r", j=PACK)
-            return dst, src
+            return dst[:, lo:hi], src[:, lo:hi]
 
         w1_bf = keep.tile([P, H * PACK], BF16, name="w1_bf", align_bytes=64)
-        w2_bf = keep.tile([P, H * PACK], BF16, name="w2_bf", align_bytes=64)
-        nc.scalar.copy(*grouped_views(w1_raw, w1_bf))
-        ew_tab = load_words("ew_tab", e_words, W, "w1_raw")
-        nc.scalar.copy(*grouped_views(w2_raw, w2_bf))
+        w2_bf = keep.tile([P, H * PACK], BF16, name="w2_bf", tag="w2_bf", align_bytes=64)
+        nc.scalar.copy(*grouped_views(w1_raw, w1_bf, 0, P // 2))
+        nc.vector.tensor_copy(*grouped_views(w1_raw, w1_bf, P // 2, P))
+        vw_tab = load_words(keep.tile([P, G], I32, name="vw_tab", tag="w1_raw", align_bytes=64), v_words)
+        nc.scalar.copy(*grouped_views(w2_raw, w2_bf, 0, P // 2))
+        nc.vector.tensor_copy(*grouped_views(w2_raw, w2_bf, P // 2, P))
 
-        def quantize(name, src, width, scales_tag):
+        def quantize(name, src, width, tag=None):
             codes = keep.tile([P, width], U32, name=name + "_codes", align_bytes=64)
-            scales = keep.tile([P, width], U8, name=name + "_scales", tag=scales_tag, align_bytes=64)
+            scales = keep.tile(
+                [P, width], U8, name=name + "_scales", tag=tag or name + "_scales", align_bytes=64
+            )
             nc.vector.quantize_mx(out=codes[:].bitcast(FP8X4), scales=scales[:], in_=src)
             return codes, scales
 
         w1_codes, w1_scales = quantize("w1", w1_bf[:], H, "es_tab")
-        vw_tab = load_words("vw_tab", v_words, G, "w1_bf")
-        w2_codes, w2_scales = quantize("w2", w2_bf[:], H, "w2_scales")
+        w2_codes, w2_scales = quantize("w2", w2_bf[:], H)
 
         for b in range(WARM_PASSES):
             idle = psum.tile([P, V], F32, name="idle", tag="y%d" % b)
@@ -125,27 +129,26 @@ def tile_picked_zfrs_silu_p_kernel(
                 stop=True,
             )
 
-        one, two = NODE_TILE, 2 * NODE_TILE
-        x_first = gather_words("x_first", xw_tab, offs_t, 0, two, "x_first")
-        e_first = gather_words("e_first", ew_tab, tok_t, 0, one, "e_first")
-        e_second = gather_words("e_second", ew_tab, tok_t, one, two, "e_second")
-        x_last = gather_words("x_last", xw_tab, offs_t, two, S, "x_last")
-        e_last = gather_words("e_last", ew_tab, tok_t, two, S, "e_last")
-        xw = [x_first[:, 0:one], x_first[:, one:two], x_last[:, 0:one], x_last[:, one:two]]
-        ew = [e_first[:], e_second[:], e_last[:, 0:one], e_last[:, one:two]]
-
         tiles = range(S // NODE_TILE)
+        xw = gather_words("xw", xw_tab, offs_t, 0, S, "w2_bf")
+        ew = [
+            gather_words("ew%d" % b, ew_tab, tok_t, b * NODE_TILE, (b + 1) * NODE_TILE)
+            for b in tiles
+        ]
+        vs = gather_scales(keep.tile([P, S], U8, name="vs", tag="slot_e", align_bytes=64), vs_tab, cand_t)
+        vw = gather_words("vw", vw_tab, cand_t, 0, V)
+
         h_bf = []
         for b in tiles:
             nodes = slice(b * NODE_TILE, (b + 1) * NODE_TILE)
-            pre = psum.tile([P, PACK, NODE_TILE], F32, name="pre", tag="pre%d" % (b % PRE_BANKS))
+            pre = psum.tile([P, PACK, NODE_TILE], F32, name="pre", tag="pre%d" % (b % 4))
             for j in range(PACK):
                 cols = slice(j * P, (j + 1) * P)
                 nc.tensor.matmul_mx(
                     out=pre[:, j, :],
                     lhsT=w1_codes[:, cols].bitcast(FP8X4),
                     lhsT_scale=w1_scales[:, cols],
-                    rhs=xw[b].bitcast(FP8X4),
+                    rhs=xw[:, nodes].bitcast(FP8X4),
                     rhs_scale=xs[X_ROW:P, nodes],
                     start=True,
                     stop=False,
@@ -154,7 +157,7 @@ def tile_picked_zfrs_silu_p_kernel(
                     out=pre[:, j, :],
                     lhsT=w2_codes[:, cols].bitcast(FP8X4),
                     lhsT_scale=w2_scales[:, cols],
-                    rhs=ew[b].bitcast(FP8X4),
+                    rhs=ew[b][:].bitcast(FP8X4),
                     rhs_scale=es[E_ROW:P, nodes],
                     start=False,
                     stop=True,
@@ -163,13 +166,10 @@ def tile_picked_zfrs_silu_p_kernel(
             nc.scalar.activation(hb[:], pre[:].rearrange("p j n -> p n j"), ACT.Silu)
             h_bf.append(hb)
 
-        vs = gather_scales("vs", vs_tab, cand_t, "w1_raw")
-        vw = gather_words("vw", vw_tab, cand_t, 0, V, "slot_vs")
-
         logits = []
         for b in tiles:
             h_codes, h_scales = quantize(
-                "h%d" % b, h_bf[b][:].rearrange("p n j -> p (n j)"), NODE_TILE, "h%d_scales" % b
+                "h%d" % b, h_bf[b][:].rearrange("p n j -> p (n j)"), NODE_TILE
             )
             y = psum.tile([P, V], F32, name="y%d" % b)
             nc.tensor.matmul_mx(

@@ -23,6 +23,8 @@ LIST_ROWS = 16
 NODE_TILE = 128
 WARM_PASSES = 3
 X_ROW, E_ROW, V_ROW = 0, 4, 8
+W1_CUT, W2_CUT = 44, 80
+KIB = 1024
 
 
 def tile_picked_zfrs_silu_p_kernel(
@@ -31,91 +33,90 @@ def tile_picked_zfrs_silu_p_kernel(
     nc = tc.nc
     with ExitStack() as ctx:
         keep = ctx.enter_context(tc.tile_pool(name="keep", bufs=1))
-        lap = ctx.enter_context(tc.tile_pool(name="lap", bufs=1))
+        shared = ctx.enter_context(tc.tile_pool(name="shared", bufs=1))
         psum = ctx.enter_context(tc.psum_pool(name="psum", bufs=1))
+
+        def own(name, shape, dtype):
+            return keep.tile(shape, dtype, name=name, align_bytes=64)
+
+        def placed(name, shape, dtype, offset):
+            return shared.tile(shape, dtype, name=name, align_bytes=64, offset=offset)
 
         def load_list(name, src):
             lst = keep.tile([P, S // LIST_ROWS], U16, name=name)
             nc.sync.dma_start(lst[:], src)
             return lst
 
-        def clear_scales(table):
+        def load_scales(table, src, row):
             nc.vector.memset(table[:].bitcast(I32), 0)
-            return table
-
-        def load_scales(table, src, row, queue, rows):
-            for r in rows:
-                queue.dma_start(
+            for r in range(PACK):
+                nc.sync.dma_start(
                     table[row + r : P : QUADRANT, :].bitcast(I32),
                     src[0, r : 16 : PACK, :].bitcast(I32),
                 )
+            return table
 
         def load_words(table, src):
             nc.sync.dma_start(table[:], src[0].rearrange("p n r -> p (n r)").bitcast(I32))
             return table
 
-        def load_weight(name, src):
-            raw = keep.tile([P, PACK, H], F32, name=name, tag=name, align_bytes=64)
+        def load_weight(raw, src):
             nc.sync.dma_start(raw[:], src.rearrange("(p r) c -> p r c", r=PACK))
             return raw
 
-        offs_t = load_list("offs_t", offs)
-        tok_t = load_list("tok_t", tok)
-        cand_t = load_list("cand_t", cand)
-        w1_raw = load_weight("w1_raw", w1)
-        w2_raw = load_weight("w2_raw", w2)
-
-        xs_tab = clear_scales(lap.tile([P, T], U8, name="xs_tab", align_bytes=64, offset=0))
-        warm_in = keep.tile([P, 1], F32, name="warm_in", tag="slot_x", align_bytes=64)
-        warm_out = keep.tile([P, 1], F32, name="warm_out", tag="slot_e", align_bytes=64)
-        nc.vector.memset(warm_in[:], 0.0)
-        es_tab = clear_scales(keep.tile([P, W], U8, name="es_tab", tag="es_tab", align_bytes=64))
-        vs_tab = clear_scales(keep.tile([P, G], U8, name="vs_tab", align_bytes=64))
-        load_scales(xs_tab, x_scales, X_ROW, nc.scalar, (0, 1, 2))
-        load_scales(xs_tab, x_scales, X_ROW, nc.gpsimd, (3,))
-        nc.scalar.activation(warm_out[:], warm_in[:], ACT.Silu)
-        load_scales(es_tab, e_scales, E_ROW, nc.scalar, (0, 1))
-        xw_tab = load_words(keep.tile([P, T], I32, name="xw_tab", tag="slot_x", align_bytes=64), x_words)
-        ew_tab = load_words(keep.tile([P, W], I32, name="ew_tab", tag="slot_e", align_bytes=64), e_words)
-        load_scales(es_tab, e_scales, E_ROW, nc.gpsimd, (2, 3))
-        load_scales(vs_tab, v_scales, V_ROW, nc.gpsimd, range(PACK))
-
-        def gather_scales(picked, table, lst):
-            nc.vector.tensor_copy(picked[:], table[:].indirect(lst[:]))
+        def gather_scales(picked, table, lst, lo=0, hi=S):
+            entries = lst[:, lo // LIST_ROWS : hi // LIST_ROWS]
+            nc.vector.tensor_copy(picked[:], table[:].indirect(entries))
             return picked
 
-        def gather_words(name, table, lst, lo, hi, tag=None):
-            picked = keep.tile([P, hi - lo], U32, name=name, tag=tag or name, align_bytes=64)
+        def gather_words(picked, table, lst, lo, hi):
             entries = lst[:, lo // LIST_ROWS : hi // LIST_ROWS]
             nc.vector.tensor_copy(picked[:], table[:].bitcast(U32).indirect(entries))
             return picked
 
-        xs = gather_scales(keep.tile([P, S], U8, name="xs", align_bytes=64), xs_tab, offs_t)
-        es = gather_scales(lap.tile([P, S], U8, name="es", align_bytes=64, offset=0), es_tab, tok_t)
+        def cast(grouped, raw, cut):
+            dst = grouped[:].rearrange("p (j m r) -> p m r j", j=PACK, r=PACK)
+            src = raw[:].rearrange("p r (m j) -> p m r j", j=PACK)
+            if cut > 0:
+                nc.scalar.copy(dst[:, :cut], src[:, :cut])
+            if cut < P:
+                nc.vector.tensor_copy(dst[:, cut:], src[:, cut:])
+            return grouped
 
-        def grouped_views(raw, grouped, lo, hi):
-            dst = grouped[:].rearrange("p (j m r) -> p m j r", j=PACK, r=PACK)
-            src = raw[:].rearrange("p r (m j) -> p m j r", j=PACK)
-            return dst[:, lo:hi], src[:, lo:hi]
-
-        w1_bf = keep.tile([P, H * PACK], BF16, name="w1_bf", align_bytes=64)
-        w2_bf = keep.tile([P, H * PACK], BF16, name="w2_bf", tag="w2_bf", align_bytes=64)
-        nc.scalar.copy(*grouped_views(w1_raw, w1_bf, 0, P // 2))
-        nc.vector.tensor_copy(*grouped_views(w1_raw, w1_bf, P // 2, P))
-        vw_tab = load_words(keep.tile([P, G], I32, name="vw_tab", tag="w1_raw", align_bytes=64), v_words)
-        nc.scalar.copy(*grouped_views(w2_raw, w2_bf, 0, P // 2))
-        nc.vector.tensor_copy(*grouped_views(w2_raw, w2_bf, P // 2, P))
-
-        def quantize(name, src, width, tag=None):
-            codes = keep.tile([P, width], U32, name=name + "_codes", align_bytes=64)
-            scales = keep.tile(
-                [P, width], U8, name=name + "_scales", tag=tag or name + "_scales", align_bytes=64
-            )
+        def quantize(name, src, scales):
+            codes = own(name, scales.shape, U32)
             nc.vector.quantize_mx(out=codes[:].bitcast(FP8X4), scales=scales[:], in_=src)
-            return codes, scales
+            return codes
 
-        w1_codes, w1_scales = quantize("w1", w1_bf[:], H, "es_tab")
-        w2_codes, w2_scales = quantize("w2", w2_bf[:], H)
+        at_w1, at_w2, at_es, at_xs, at_ew, at_bf = 0, 8 * KIB, 16 * KIB, 17 * KIB, 19 * KIB, 28 * KIB
+
+        offs_t = load_list("offs_t", offs)
+        tok_t = load_list("tok_t", tok)
+        cand_t = load_list("cand_t", cand)
+        ew_tab = load_words(placed("ew_tab", [P, W], I32, at_ew), e_words)
+        xs_tab = load_scales(own("xs_tab", [P, T], U8), x_scales, X_ROW)
+
+        warm_in = placed("warm_in", [P, 32], F32, at_w2 - 64)
+        warm_out = placed("warm_out", [P, 32], F32, at_es)
+        nc.vector.memset(warm_in[:], 0.0)
+        nc.scalar.activation(warm_out[:], warm_in[:], ACT.Silu)
+        w1_raw = load_weight(placed("w1_raw", [P, PACK, H], F32, at_w1), w1)
+        w2_raw = load_weight(placed("w2_raw", [P, PACK, H], F32, at_w2), w2)
+        es_tab = load_scales(placed("es_tab", [P, W], U8, at_es), e_scales, E_ROW)
+
+        ew = gather_words(own("ew", [P, S], U32), ew_tab, tok_t, 0, S)
+        xs = gather_scales(own("xs", [P, S], U8), xs_tab, offs_t)
+        xw_tab = load_words(placed("xw_tab", [P, T], I32, at_ew + KIB), x_words)
+
+        w1_bf = cast(placed("w1_bf", [P, H * PACK], BF16, at_bf), w1_raw, W1_CUT)
+        vw_tab = load_words(placed("vw_tab", [P, G], I32, at_w1), v_words)
+        w1_scales = own("w1_scales", [P, H], U8)
+        w1_codes = quantize("w1_codes", w1_bf[:], w1_scales)
+        vs_tab = load_scales(placed("vs_tab", [P, G], U8, at_bf), v_scales, V_ROW)
+        w2_bf = cast(own("w2_bf", [P, H * PACK], BF16), w2_raw, W2_CUT)
+        es = gather_scales(own("es", [P, S], U8), es_tab, tok_t)
+        w2_scales = placed("w2_scales", [P, H], U8, at_es)
+        w2_codes = quantize("w2_codes", w2_bf[:], w2_scales)
 
         for b in range(WARM_PASSES):
             idle = psum.tile([P, V], F32, name="idle", tag="y%d" % b)
@@ -123,54 +124,54 @@ def tile_picked_zfrs_silu_p_kernel(
                 out=idle[:],
                 lhsT=w1_codes[:, 0:P].bitcast(FP8X4),
                 lhsT_scale=w1_scales[:, 0:P],
-                rhs=w2_codes[:].bitcast(FP8X4),
-                rhs_scale=w2_scales[:],
+                rhs=ew[:].bitcast(FP8X4),
+                rhs_scale=es[E_ROW:P, :],
                 start=True,
                 stop=True,
             )
 
-        tiles = range(S // NODE_TILE)
-        xw = gather_words("xw", xw_tab, offs_t, 0, S, "w2_bf")
-        ew = [
-            gather_words("ew%d" % b, ew_tab, tok_t, b * NODE_TILE, (b + 1) * NODE_TILE)
-            for b in tiles
+        half = S // 2
+        xw = [
+            gather_words(own("xw%d" % u, [P, half], U32), xw_tab, offs_t, u * half, (u + 1) * half)
+            for u in range(2)
         ]
-        vs = gather_scales(keep.tile([P, S], U8, name="vs", tag="slot_e", align_bytes=64), vs_tab, cand_t)
-        vw = gather_words("vw", vw_tab, cand_t, 0, V)
+        vw = gather_words(own("vw", [P, V], U32), vw_tab, cand_t, 0, V)
+        vs = gather_scales(own("vs", [P, V], U8), vs_tab, cand_t, 0, V)
 
+        tiles = range(S // NODE_TILE)
         h_bf = []
         for b in tiles:
             nodes = slice(b * NODE_TILE, (b + 1) * NODE_TILE)
-            pre = psum.tile([P, PACK, NODE_TILE], F32, name="pre", tag="pre%d" % (b % 4))
+            in_half = slice(b % 2 * NODE_TILE, (b % 2 + 1) * NODE_TILE)
+            pre = psum.tile([P, PACK, NODE_TILE], F32, name="pre", tag="pre%d" % (b % 2))
             for j in range(PACK):
                 cols = slice(j * P, (j + 1) * P)
                 nc.tensor.matmul_mx(
                     out=pre[:, j, :],
-                    lhsT=w1_codes[:, cols].bitcast(FP8X4),
-                    lhsT_scale=w1_scales[:, cols],
-                    rhs=xw[:, nodes].bitcast(FP8X4),
-                    rhs_scale=xs[X_ROW:P, nodes],
+                    lhsT=w2_codes[:, cols].bitcast(FP8X4),
+                    lhsT_scale=w2_scales[:, cols],
+                    rhs=ew[:, nodes].bitcast(FP8X4),
+                    rhs_scale=es[E_ROW:P, nodes],
                     start=True,
                     stop=False,
                 )
                 nc.tensor.matmul_mx(
                     out=pre[:, j, :],
-                    lhsT=w2_codes[:, cols].bitcast(FP8X4),
-                    lhsT_scale=w2_scales[:, cols],
-                    rhs=ew[b][:].bitcast(FP8X4),
-                    rhs_scale=es[E_ROW:P, nodes],
+                    lhsT=w1_codes[:, cols].bitcast(FP8X4),
+                    lhsT_scale=w1_scales[:, cols],
+                    rhs=xw[b // 2][:, in_half].bitcast(FP8X4),
+                    rhs_scale=xs[X_ROW:P, nodes],
                     start=False,
                     stop=True,
                 )
-            hb = keep.tile([P, NODE_TILE, PACK], BF16, name="h_bf%d" % b, align_bytes=64)
+            hb = own("h_bf%d" % b, [P, NODE_TILE, PACK], BF16)
             nc.scalar.activation(hb[:], pre[:].rearrange("p j n -> p n j"), ACT.Silu)
             h_bf.append(hb)
 
         logits = []
         for b in tiles:
-            h_codes, h_scales = quantize(
-                "h%d" % b, h_bf[b][:].rearrange("p n j -> p (n j)"), NODE_TILE
-            )
+            h_scales = placed("h%d_scales" % b, [P, NODE_TILE], U8, (at_xs if b < 0 else at_bf) + b * NODE_TILE)
+            h_codes = quantize("h%d_codes" % b, h_bf[b][:].rearrange("p n j -> p (n j)"), h_scales)
             y = psum.tile([P, V], F32, name="y%d" % b)
             nc.tensor.matmul_mx(
                 out=y[:],
@@ -183,19 +184,32 @@ def tile_picked_zfrs_silu_p_kernel(
             )
             logits.append(y)
 
-        neg_max = []
-        for b in tiles:
-            lowest = keep.tile([P, 1], F32, name="neg_max%d" % b)
+        def row_max(b, offset):
+            lowest = placed("neg_max%d" % b, [P, 1], F32, offset)
             nc.vector.tensor_reduce(lowest[:], logits[b][:], AX.X, ALU.max, negate=True)
-            neg_max.append(lowest)
-        for b in tiles:
-            ex = keep.tile([P, V], F32, name="ex%d" % b)
-            total = keep.tile([P, 1], F32, name="total%d" % b)
+            return lowest
+
+        def exp_and_sum(b):
+            ex = own("ex%d" % b, [P, V], F32)
+            total = own("total%d" % b, [P, 1], F32)
             nc.scalar.activation(
                 ex[:], logits[b][:], ACT.Exp, bias=neg_max[b][:], accum_out=total[:]
             )
-            inv = keep.tile([P, 1], F32, name="inv%d" % b)
+            inv = own("inv%d" % b, [P, 1], F32)
             nc.vector.reciprocal(inv[:], total[:])
-            res = keep.tile([P, V], F32, name="res%d" % b)
+            return ex, inv
+
+        def scale_and_store(b, res, ex, inv):
             nc.vector.tensor_scalar(res[:], ex[:], inv[:], None, ALU.mult)
             nc.sync.dma_start(out[b * NODE_TILE : (b + 1) * NODE_TILE, :], res[:])
+
+        at_max = 36 * KIB
+        neg_max = [row_max(0, at_max), row_max(1, at_max + 64), row_max(2, at_max + 128)]
+        first = exp_and_sum(0)
+        neg_max.append(row_max(3, at_max))
+        scale_and_store(0, own("res0", [P, V], F32), *first)
+        second = exp_and_sum(1)
+        third = exp_and_sum(2)
+        scale_and_store(1, placed("res1", [P, V], F32, at_max + 128), *second)
+        scale_and_store(2, own("res2", [P, V], F32), *third)
+        scale_and_store(3, own("res3", [P, V], F32), *exp_and_sum(3))

@@ -23,7 +23,7 @@ LIST_ROWS = 16
 NODE_TILE = 128
 WARM_PASSES = 3
 X_ROW, E_ROW, V_ROW = 0, 4, 8
-W1_CUT, W2_CUT = 44, 80
+W1_CUT, W2_CUT = 64, 96
 KIB = 1024
 
 
@@ -88,13 +88,13 @@ def tile_picked_zfrs_silu_p_kernel(
             nc.vector.quantize_mx(out=codes[:].bitcast(FP8X4), scales=scales[:], in_=src)
             return codes
 
-        at_w1, at_w2, at_es, at_xs, at_ew, at_bf = 0, 8 * KIB, 16 * KIB, 17 * KIB, 19 * KIB, 28 * KIB
+        at_w1, at_w2, at_es, at_xs, at_ew, at_bf = 0, 8 * KIB, 16 * KIB, 17 * KIB, 19 * KIB, 0
 
         offs_t = load_list("offs_t", offs)
         tok_t = load_list("tok_t", tok)
         cand_t = load_list("cand_t", cand)
         ew_tab = load_words(placed("ew_tab", [P, W], I32, at_ew), e_words)
-        xs_tab = load_scales(own("xs_tab", [P, T], U8), x_scales, X_ROW)
+        xs_tab = load_scales(placed("xs_tab", [P, T], U8, at_xs), x_scales, X_ROW)
 
         warm_in = placed("warm_in", [P, 32], F32, at_w2 - 64)
         warm_out = placed("warm_out", [P, 32], F32, at_es)
@@ -105,14 +105,14 @@ def tile_picked_zfrs_silu_p_kernel(
         es_tab = load_scales(placed("es_tab", [P, W], U8, at_es), e_scales, E_ROW)
 
         ew = gather_words(own("ew", [P, S], U32), ew_tab, tok_t, 0, S)
+        xw_tab = load_words(placed("xw_tab", [P, T], I32, at_ew), x_words)
         xs = gather_scales(own("xs", [P, S], U8), xs_tab, offs_t)
-        xw_tab = load_words(placed("xw_tab", [P, T], I32, at_ew + KIB), x_words)
+        vs_tab = load_scales(placed("vs_tab", [P, G], U8, at_xs), v_scales, V_ROW)
 
-        w1_bf = cast(placed("w1_bf", [P, H * PACK], BF16, at_bf), w1_raw, W1_CUT)
+        w1_bf = cast(own("w1_bf", [P, H * PACK], BF16), w1_raw, W1_CUT)
         vw_tab = load_words(placed("vw_tab", [P, G], I32, at_w1), v_words)
         w1_scales = own("w1_scales", [P, H], U8)
         w1_codes = quantize("w1_codes", w1_bf[:], w1_scales)
-        vs_tab = load_scales(placed("vs_tab", [P, G], U8, at_bf), v_scales, V_ROW)
         w2_bf = cast(own("w2_bf", [P, H * PACK], BF16), w2_raw, W2_CUT)
         es = gather_scales(own("es", [P, S], U8), es_tab, tok_t)
         w2_scales = placed("w2_scales", [P, H], U8, at_es)
@@ -135,15 +135,15 @@ def tile_picked_zfrs_silu_p_kernel(
             gather_words(own("xw%d" % u, [P, half], U32), xw_tab, offs_t, u * half, (u + 1) * half)
             for u in range(2)
         ]
-        vw = gather_words(own("vw", [P, V], U32), vw_tab, cand_t, 0, V)
         vs = gather_scales(own("vs", [P, V], U8), vs_tab, cand_t, 0, V)
+        vw = gather_words(own("vw", [P, V], U32), vw_tab, cand_t, 0, V)
 
         tiles = range(S // NODE_TILE)
         h_bf = []
         for b in tiles:
             nodes = slice(b * NODE_TILE, (b + 1) * NODE_TILE)
             in_half = slice(b % 2 * NODE_TILE, (b % 2 + 1) * NODE_TILE)
-            pre = psum.tile([P, PACK, NODE_TILE], F32, name="pre", tag="pre%d" % (b % 2))
+            pre = psum.tile([P, PACK, NODE_TILE], F32, name="pre", tag="pre%d" % (b % 3))
             for j in range(PACK):
                 cols = slice(j * P, (j + 1) * P)
                 nc.tensor.matmul_mx(
@@ -170,7 +170,7 @@ def tile_picked_zfrs_silu_p_kernel(
 
         logits = []
         for b in tiles:
-            h_scales = placed("h%d_scales" % b, [P, NODE_TILE], U8, (at_xs if b < 0 else at_bf) + b * NODE_TILE)
+            h_scales = placed("h%d_scales" % b, [P, NODE_TILE], U8, at_bf + b * NODE_TILE) if b >= 0 else placed("h%d_scales" % b, [P, NODE_TILE], U8, at_xs + b * NODE_TILE)
             h_codes = quantize("h%d_codes" % b, h_bf[b][:].rearrange("p n j -> p (n j)"), h_scales)
             y = psum.tile([P, V], F32, name="y%d" % b)
             nc.tensor.matmul_mx(

@@ -21,9 +21,8 @@ PACK = 4
 QUADRANT = 32
 LIST_ROWS = 16
 NODE_TILE = 128
-WARM_PASSES = 3
 X_ROW, E_ROW, V_ROW = 0, 4, 8
-W1_CUT, W2_CUT = 64, 96
+W1_CUT, W2_CUT = 64, 44
 KIB = 1024
 
 
@@ -88,44 +87,40 @@ def tile_picked_zfrs_silu_p_kernel(
             nc.vector.quantize_mx(out=codes[:].bitcast(FP8X4), scales=scales[:], in_=src)
             return codes
 
-        at_w1, at_w2, at_es, at_xs, at_ew, at_bf = 0, 8 * KIB, 16 * KIB, 17 * KIB, 19 * KIB, 0
+        at_bf, at_xs = 0, 0
 
-        offs_t = load_list("offs_t", offs)
         tok_t = load_list("tok_t", tok)
+        ew_tab = load_words(own("ew_tab", [P, W], I32), e_words)
+        offs_t = load_list("offs_t", offs)
+        xs_tab = load_scales(own("xs_tab", [P, T], U8), x_scales, X_ROW)
+        w1_raw = load_weight(own("w1_raw", [P, PACK, H], F32), w1)
+        es_tab = load_scales(own("es_tab", [P, W], U8), e_scales, E_ROW)
+        w2_raw = load_weight(own("w2_raw", [P, PACK, H], F32), w2)
         cand_t = load_list("cand_t", cand)
-        ew_tab = load_words(placed("ew_tab", [P, W], I32, at_ew), e_words)
-        xs_tab = load_scales(placed("xs_tab", [P, T], U8, at_xs), x_scales, X_ROW)
-
-        warm_in = placed("warm_in", [P, 32], F32, at_w2 - 64)
-        warm_out = placed("warm_out", [P, 32], F32, at_es)
-        nc.vector.memset(warm_in[:], 0.0)
-        nc.scalar.activation(warm_out[:], warm_in[:], ACT.Silu)
-        w1_raw = load_weight(placed("w1_raw", [P, PACK, H], F32, at_w1), w1)
-        w2_raw = load_weight(placed("w2_raw", [P, PACK, H], F32, at_w2), w2)
-        es_tab = load_scales(placed("es_tab", [P, W], U8, at_es), e_scales, E_ROW)
+        xw_tab = load_words(own("xw_tab", [P, T], I32), x_words)
+        vs_tab = load_scales(own("vs_tab", [P, G], U8), v_scales, V_ROW)
+        vw_tab = load_words(placed("vw_tab", [P, G], I32, at_bf), v_words)
 
         ew = gather_words(own("ew", [P, S], U32), ew_tab, tok_t, 0, S)
-        xw_tab = load_words(placed("xw_tab", [P, T], I32, at_ew), x_words)
         xs = gather_scales(own("xs", [P, S], U8), xs_tab, offs_t)
-        vs_tab = load_scales(placed("vs_tab", [P, G], U8, at_xs), v_scales, V_ROW)
-
         w1_bf = cast(own("w1_bf", [P, H * PACK], BF16), w1_raw, W1_CUT)
-        vw_tab = load_words(placed("vw_tab", [P, G], I32, at_w1), v_words)
+        es = gather_scales(own("es", [P, S], U8), es_tab, tok_t)
         w1_scales = own("w1_scales", [P, H], U8)
         w1_codes = quantize("w1_codes", w1_bf[:], w1_scales)
         w2_bf = cast(own("w2_bf", [P, H * PACK], BF16), w2_raw, W2_CUT)
-        es = gather_scales(own("es", [P, S], U8), es_tab, tok_t)
-        w2_scales = placed("w2_scales", [P, H], U8, at_es)
+        w2_scales = own("w2_scales", [P, H], U8)
         w2_codes = quantize("w2_codes", w2_bf[:], w2_scales)
 
-        for b in range(WARM_PASSES):
+        for b, (codes, scales) in enumerate(
+            [(ew, es[E_ROW:P, :]), (ew, es[E_ROW:P, :]), (w2_codes, w2_scales[:])]
+        ):
             idle = psum.tile([P, V], F32, name="idle", tag="y%d" % b)
             nc.tensor.matmul_mx(
                 out=idle[:],
                 lhsT=w1_codes[:, 0:P].bitcast(FP8X4),
                 lhsT_scale=w1_scales[:, 0:P],
-                rhs=ew[:].bitcast(FP8X4),
-                rhs_scale=es[E_ROW:P, :],
+                rhs=codes[:].bitcast(FP8X4),
+                rhs_scale=scales,
                 start=True,
                 stop=True,
             )

@@ -19,11 +19,16 @@ AX = mybir.AxisListType
 P = 128
 PACK = 4
 QUADRANT = 32
+BLOCKS = K // 32
 LIST_ROWS = 16
+ALIGN = 64
 NODE_TILE = 128
+X_PIECE = 256
+PRE_BANKS = 3
 X_ROW, E_ROW, V_ROW = 0, 4, 8
-W1_CUT, W2_CUT = 64, 44
-KIB = 1024
+W1_ON_SCALAR, W2_ON_SCALAR = 64, 44
+V_WORDS_AT = 0
+MAXIMA_AT = V_WORDS_AT + 4 * G
 
 
 def tile_picked_zfrs_silu_p_kernel(
@@ -36,10 +41,10 @@ def tile_picked_zfrs_silu_p_kernel(
         psum = ctx.enter_context(tc.psum_pool(name="psum", bufs=1))
 
         def own(name, shape, dtype):
-            return keep.tile(shape, dtype, name=name, align_bytes=64)
+            return keep.tile(shape, dtype, name=name, align_bytes=ALIGN)
 
         def placed(name, shape, dtype, offset):
-            return shared.tile(shape, dtype, name=name, align_bytes=64, offset=offset)
+            return shared.tile(shape, dtype, name=name, align_bytes=ALIGN, offset=offset)
 
         def load_list(name, src):
             lst = keep.tile([P, S // LIST_ROWS], U16, name=name)
@@ -51,7 +56,7 @@ def tile_picked_zfrs_silu_p_kernel(
             for r in range(PACK):
                 nc.sync.dma_start(
                     table[row + r : P : QUADRANT, :].bitcast(I32),
-                    src[0, r : 16 : PACK, :].bitcast(I32),
+                    src[0, r:BLOCKS:PACK, :].bitcast(I32),
                 )
             return table
 
@@ -63,23 +68,19 @@ def tile_picked_zfrs_silu_p_kernel(
             nc.sync.dma_start(raw[:], src.rearrange("(p r) c -> p r c", r=PACK))
             return raw
 
-        def gather_scales(picked, table, lst, lo=0, hi=S):
-            entries = lst[:, lo // LIST_ROWS : hi // LIST_ROWS]
-            nc.vector.tensor_copy(picked[:], table[:].indirect(entries))
+        def gather_scales(picked, table, lst):
+            nc.vector.tensor_copy(picked[:], table[:].indirect(lst[:]))
             return picked
 
-        def gather_words(picked, table, lst, lo, hi):
-            entries = lst[:, lo // LIST_ROWS : hi // LIST_ROWS]
+        def gather_words(picked, table, entries):
             nc.vector.tensor_copy(picked[:], table[:].bitcast(U32).indirect(entries))
             return picked
 
-        def cast(grouped, raw, cut):
+        def cast(grouped, raw, on_scalar):
             dst = grouped[:].rearrange("p (j m r) -> p m r j", j=PACK, r=PACK)
             src = raw[:].rearrange("p r (m j) -> p m r j", j=PACK)
-            if cut > 0:
-                nc.scalar.copy(dst[:, :cut], src[:, :cut])
-            if cut < P:
-                nc.vector.tensor_copy(dst[:, cut:], src[:, cut:])
+            nc.scalar.copy(dst[:, :on_scalar], src[:, :on_scalar])
+            nc.vector.tensor_copy(dst[:, on_scalar:], src[:, on_scalar:])
             return grouped
 
         def quantize(name, src, scales):
@@ -87,33 +88,30 @@ def tile_picked_zfrs_silu_p_kernel(
             nc.vector.quantize_mx(out=codes[:].bitcast(FP8X4), scales=scales[:], in_=src)
             return codes
 
-        at_bf, at_xs = 0, 0
-
-        tok_t = load_list("tok_t", tok)
         ew_tab = load_words(own("ew_tab", [P, W], I32), e_words)
-        offs_t = load_list("offs_t", offs)
-        xs_tab = load_scales(own("xs_tab", [P, T], U8), x_scales, X_ROW)
-        w1_raw = load_weight(own("w1_raw", [P, PACK, H], F32), w1)
+        tok_t = load_list("tok_t", tok)
         es_tab = load_scales(own("es_tab", [P, W], U8), e_scales, E_ROW)
+        offs_t = load_list("offs_t", offs)
+        w1_raw = load_weight(own("w1_raw", [P, PACK, H], F32), w1)
+        xs_tab = load_scales(own("xs_tab", [P, T], U8), x_scales, X_ROW)
         w2_raw = load_weight(own("w2_raw", [P, PACK, H], F32), w2)
-        cand_t = load_list("cand_t", cand)
         xw_tab = load_words(own("xw_tab", [P, T], I32), x_words)
+        cand_t = load_list("cand_t", cand)
         vs_tab = load_scales(own("vs_tab", [P, G], U8), v_scales, V_ROW)
-        vw_tab = load_words(placed("vw_tab", [P, G], I32, at_bf), v_words)
+        vw_tab = load_words(placed("vw_tab", [P, G], I32, V_WORDS_AT), v_words)
 
-        ew = gather_words(own("ew", [P, S], U32), ew_tab, tok_t, 0, S)
-        xs = gather_scales(own("xs", [P, S], U8), xs_tab, offs_t)
-        w1_bf = cast(own("w1_bf", [P, H * PACK], BF16), w1_raw, W1_CUT)
+        ew = gather_words(own("ew", [P, S], U32), ew_tab, tok_t[:])
         es = gather_scales(own("es", [P, S], U8), es_tab, tok_t)
+        w1_bf = cast(own("w1_bf", [P, H * PACK], BF16), w1_raw, W1_ON_SCALAR)
+        xs = gather_scales(own("xs", [P, S], U8), xs_tab, offs_t)
         w1_scales = own("w1_scales", [P, H], U8)
         w1_codes = quantize("w1_codes", w1_bf[:], w1_scales)
-        w2_bf = cast(own("w2_bf", [P, H * PACK], BF16), w2_raw, W2_CUT)
+        w2_bf = cast(own("w2_bf", [P, H * PACK], BF16), w2_raw, W2_ON_SCALAR)
         w2_scales = own("w2_scales", [P, H], U8)
         w2_codes = quantize("w2_codes", w2_bf[:], w2_scales)
 
-        for b, (codes, scales) in enumerate(
-            [(ew, es[E_ROW:P, :]), (ew, es[E_ROW:P, :]), (w2_codes, w2_scales[:])]
-        ):
+        after_w1, after_w2 = (ew, es[E_ROW:P, :]), (w2_codes, w2_scales[:])
+        for b, (codes, scales) in enumerate([after_w1, after_w1, after_w2]):
             idle = psum.tile([P, V], F32, name="idle", tag="y%d" % b)
             nc.tensor.matmul_mx(
                 out=idle[:],
@@ -125,20 +123,25 @@ def tile_picked_zfrs_silu_p_kernel(
                 stop=True,
             )
 
-        half = S // 2
+        piece_cols = X_PIECE // LIST_ROWS
         xw = [
-            gather_words(own("xw%d" % u, [P, half], U32), xw_tab, offs_t, u * half, (u + 1) * half)
-            for u in range(2)
+            gather_words(
+                own("xw%d" % u, [P, X_PIECE], U32),
+                xw_tab,
+                offs_t[:, u * piece_cols : (u + 1) * piece_cols],
+            )
+            for u in range(S // X_PIECE)
         ]
-        vs = gather_scales(own("vs", [P, V], U8), vs_tab, cand_t, 0, V)
-        vw = gather_words(own("vw", [P, V], U32), vw_tab, cand_t, 0, V)
+        vs = gather_scales(own("vs", [P, V], U8), vs_tab, cand_t)
+        vw = gather_words(own("vw", [P, V], U32), vw_tab, cand_t[:])
 
         tiles = range(S // NODE_TILE)
         h_bf = []
         for b in tiles:
             nodes = slice(b * NODE_TILE, (b + 1) * NODE_TILE)
-            in_half = slice(b % 2 * NODE_TILE, (b % 2 + 1) * NODE_TILE)
-            pre = psum.tile([P, PACK, NODE_TILE], F32, name="pre", tag="pre%d" % (b % 3))
+            piece, first = divmod(b * NODE_TILE, X_PIECE)
+            in_piece = slice(first, first + NODE_TILE)
+            pre = psum.tile([P, PACK, NODE_TILE], F32, name="pre", tag="pre%d" % (b % PRE_BANKS))
             for j in range(PACK):
                 cols = slice(j * P, (j + 1) * P)
                 nc.tensor.matmul_mx(
@@ -154,7 +157,7 @@ def tile_picked_zfrs_silu_p_kernel(
                     out=pre[:, j, :],
                     lhsT=w1_codes[:, cols].bitcast(FP8X4),
                     lhsT_scale=w1_scales[:, cols],
-                    rhs=xw[b // 2][:, in_half].bitcast(FP8X4),
+                    rhs=xw[piece][:, in_piece].bitcast(FP8X4),
                     rhs_scale=xs[X_ROW:P, nodes],
                     start=False,
                     stop=True,
@@ -165,7 +168,7 @@ def tile_picked_zfrs_silu_p_kernel(
 
         logits = []
         for b in tiles:
-            h_scales = placed("h%d_scales" % b, [P, NODE_TILE], U8, at_bf + b * NODE_TILE) if b >= 0 else placed("h%d_scales" % b, [P, NODE_TILE], U8, at_xs + b * NODE_TILE)
+            h_scales = placed("h%d_scales" % b, [P, NODE_TILE], U8, V_WORDS_AT + b * NODE_TILE)
             h_codes = quantize("h%d_codes" % b, h_bf[b][:].rearrange("p n j -> p (n j)"), h_scales)
             y = psum.tile([P, V], F32, name="y%d" % b)
             nc.tensor.matmul_mx(
@@ -179,12 +182,15 @@ def tile_picked_zfrs_silu_p_kernel(
             )
             logits.append(y)
 
-        def row_max(b, offset):
-            lowest = placed("neg_max%d" % b, [P, 1], F32, offset)
-            nc.vector.tensor_reduce(lowest[:], logits[b][:], AX.X, ALU.max, negate=True)
-            return lowest
+        def max_at(b):
+            return MAXIMA_AT + b * ALIGN
 
-        def exp_and_sum(b):
+        def negated_max(b, offset):
+            neg = placed("neg_max%d" % b, [P, 1], F32, offset)
+            nc.vector.tensor_reduce(neg[:], logits[b][:], AX.X, ALU.max, negate=True)
+            return neg
+
+        def exp_and_inverse_sum(b):
             ex = own("ex%d" % b, [P, V], F32)
             total = own("total%d" % b, [P, 1], F32)
             nc.scalar.activation(
@@ -198,13 +204,12 @@ def tile_picked_zfrs_silu_p_kernel(
             nc.vector.tensor_scalar(res[:], ex[:], inv[:], None, ALU.mult)
             nc.sync.dma_start(out[b * NODE_TILE : (b + 1) * NODE_TILE, :], res[:])
 
-        at_max = 36 * KIB
-        neg_max = [row_max(0, at_max), row_max(1, at_max + 64), row_max(2, at_max + 128)]
-        first = exp_and_sum(0)
-        neg_max.append(row_max(3, at_max))
-        scale_and_store(0, own("res0", [P, V], F32), *first)
-        second = exp_and_sum(1)
-        third = exp_and_sum(2)
-        scale_and_store(1, placed("res1", [P, V], F32, at_max + 128), *second)
-        scale_and_store(2, own("res2", [P, V], F32), *third)
-        scale_and_store(3, own("res3", [P, V], F32), *exp_and_sum(3))
+        neg_max = [negated_max(b, max_at(b)) for b in range(3)]
+        parts_0 = exp_and_inverse_sum(0)
+        neg_max.append(negated_max(3, max_at(0)))
+        scale_and_store(0, own("res0", [P, V], F32), *parts_0)
+        parts_1 = exp_and_inverse_sum(1)
+        parts_2 = exp_and_inverse_sum(2)
+        scale_and_store(1, placed("res1", [P, V], F32, max_at(2)), *parts_1)
+        scale_and_store(2, own("res2", [P, V], F32), *parts_2)
+        scale_and_store(3, own("res3", [P, V], F32), *exp_and_inverse_sum(3))

@@ -23,10 +23,11 @@ BLOCKS = K // 32
 LIST_ROWS = 16
 ALIGN = 64
 NODE_TILE = 128
-X_PIECE = 256
+X_PIECES = (1, 1, 2)
+E_ROW = 4
 PRE_BANKS = 3
-X_ROW, E_ROW, V_ROW = 0, 4, 8
-W1_ON_SCALAR, W2_ON_SCALAR = 64, 44
+TABLE_STEP = P // BLOCKS
+W2_ON_SCALAR, W1_ON_SCALAR = 128, 50
 V_WORDS_AT = 0
 MAXIMA_AT = V_WORDS_AT + 4 * G
 
@@ -51,7 +52,12 @@ def tile_picked_zfrs_silu_p_kernel(
             nc.sync.dma_start(lst[:], src)
             return lst
 
-        def load_scales(table, src, row):
+        def load_scales(table, src, queue):
+            nc.vector.memset(table[:].bitcast(I32), 0)
+            queue.dma_start(table[0:P:TABLE_STEP, :].bitcast(I32), src[0].bitcast(I32))
+            return table
+
+        def load_plane(table, src, row):
             nc.vector.memset(table[:].bitcast(I32), 0)
             for r in range(PACK):
                 nc.sync.dma_start(
@@ -59,6 +65,19 @@ def tile_picked_zfrs_silu_p_kernel(
                     src[0, r:BLOCKS:PACK, :].bitcast(I32),
                 )
             return table
+
+        def cleared_plane(name):
+            plane = own(name, [P, S], U8)
+            nc.vector.memset(plane[:].bitcast(I32), 0)
+            return plane
+
+        def place_scales(plane, picked):
+            for r in range(PACK):
+                nc.sync.dma_start(
+                    plane[r:P:QUADRANT, :].bitcast(I32),
+                    picked[r * TABLE_STEP : P : QUADRANT, :].bitcast(I32),
+                )
+            return plane
 
         def load_words(table, src):
             nc.sync.dma_start(table[:], src[0].rearrange("p n r -> p (n r)").bitcast(I32))
@@ -76,11 +95,12 @@ def tile_picked_zfrs_silu_p_kernel(
             nc.vector.tensor_copy(picked[:], table[:].bitcast(U32).indirect(entries))
             return picked
 
-        def cast(grouped, raw, on_scalar):
-            dst = grouped[:].rearrange("p (j m r) -> p m r j", j=PACK, r=PACK)
-            src = raw[:].rearrange("p r (m j) -> p m r j", j=PACK)
+        def cast(grouped, raw, on_scalar, js):
+            dst = grouped[:].rearrange("p (j m r) -> p m r j", m=P, r=PACK)
+            src = raw[:].rearrange("p r (m j) -> p m r j", j=PACK)[:, :, :, js]
             nc.scalar.copy(dst[:, :on_scalar], src[:, :on_scalar])
-            nc.vector.tensor_copy(dst[:, on_scalar:], src[:, on_scalar:])
+            if on_scalar < P:
+                nc.vector.tensor_copy(dst[:, on_scalar:], src[:, on_scalar:])
             return grouped
 
         def quantize(name, src, scales):
@@ -90,80 +110,87 @@ def tile_picked_zfrs_silu_p_kernel(
 
         ew_tab = load_words(own("ew_tab", [P, W], I32), e_words)
         tok_t = load_list("tok_t", tok)
-        es_tab = load_scales(own("es_tab", [P, W], U8), e_scales, E_ROW)
+        es_tab = load_plane(own("es_tab", [P, W], U8), e_scales, E_ROW)
         offs_t = load_list("offs_t", offs)
-        w1_raw = load_weight(own("w1_raw", [P, PACK, H], F32), w1)
-        xs_tab = load_scales(own("xs_tab", [P, T], U8), x_scales, X_ROW)
         w2_raw = load_weight(own("w2_raw", [P, PACK, H], F32), w2)
-        xw_tab = load_words(own("xw_tab", [P, T], I32), x_words)
+        xs_tab = load_scales(own("xs_tab", [P, T], U8), x_scales, nc.sync)
         cand_t = load_list("cand_t", cand)
-        vs_tab = load_scales(own("vs_tab", [P, G], U8), v_scales, V_ROW)
-        vw_tab = load_words(placed("vw_tab", [P, G], I32, V_WORDS_AT), v_words)
+        vs_tab = load_scales(own("vs_tab", [P, G], U8), v_scales, nc.sync)
+        w1_raw = load_weight(own("w1_raw", [P, PACK, H], F32), w1)
+        xs, vs = [cleared_plane(name) for name in ("xs", "vs")]
 
         ew = gather_words(own("ew", [P, S], U32), ew_tab, tok_t[:])
         es = gather_scales(own("es", [P, S], U8), es_tab, tok_t)
-        w1_bf = cast(own("w1_bf", [P, H * PACK], BF16), w1_raw, W1_ON_SCALAR)
-        xs = gather_scales(own("xs", [P, S], U8), xs_tab, offs_t)
-        w1_scales = own("w1_scales", [P, H], U8)
-        w1_codes = quantize("w1_codes", w1_bf[:], w1_scales)
-        w2_bf = cast(own("w2_bf", [P, H * PACK], BF16), w2_raw, W2_ON_SCALAR)
+        xw_tab = load_words(own("xw_tab", [P, T], I32), x_words)
+        xs_picked = gather_scales(own("xs_picked", [P, S], U8), xs_tab, offs_t)
+        place_scales(xs, xs_picked)
+        vw_tab = load_words(placed("vw_tab", [P, G], I32, V_WORDS_AT), v_words)
+        vs_picked = gather_scales(own("vs_picked", [P, V], U8), vs_tab, cand_t)
+        place_scales(vs, vs_picked)
+
+        w2_bf = cast(own("w2_bf", [P, H * PACK], BF16), w2_raw, W2_ON_SCALAR, slice(0, PACK))
         w2_scales = own("w2_scales", [P, H], U8)
         w2_codes = quantize("w2_codes", w2_bf[:], w2_scales)
-
-        after_w1, after_w2 = (ew, es[E_ROW:P, :]), (w2_codes, w2_scales[:])
-        for b, (codes, scales) in enumerate([after_w1, after_w1, after_w2]):
-            idle = psum.tile([P, V], F32, name="idle", tag="y%d" % b)
-            nc.tensor.matmul_mx(
-                out=idle[:],
-                lhsT=w1_codes[:, 0:P].bitcast(FP8X4),
-                lhsT_scale=w1_scales[:, 0:P],
-                rhs=codes[:].bitcast(FP8X4),
-                rhs_scale=scales,
-                start=True,
-                stop=True,
-            )
-
-        piece_cols = X_PIECE // LIST_ROWS
-        xw = [
-            gather_words(
-                own("xw%d" % u, [P, X_PIECE], U32),
-                xw_tab,
-                offs_t[:, u * piece_cols : (u + 1) * piece_cols],
-            )
-            for u in range(S // X_PIECE)
-        ]
-        vs = gather_scales(own("vs", [P, V], U8), vs_tab, cand_t)
-        vw = gather_words(own("vw", [P, V], U32), vw_tab, cand_t[:])
+        w1_codes, w1_scales = [], []
+        halves = [cast(own("w1_bf%d" % u, [P, H * PACK // 2], BF16), w1_raw, share, slice(2 * u, 2 * u + 2))
+                  for u, share in enumerate((P, W1_ON_SCALAR))]
+        for u, half in enumerate(halves):
+            scales = own("w1_scales%d" % u, [P, H // 2], U8)
+            codes = quantize("w1_codes%d" % u, half[:], scales)
+            w1_scales.extend([scales[:, 0:P], scales[:, P : 2 * P]])
+            w1_codes.extend([codes[:, 0:P], codes[:, P : 2 * P]])
 
         tiles = range(S // NODE_TILE)
-        h_bf = []
-        for b in tiles:
+        pre = []
+
+        def passes_over_e(b):
             nodes = slice(b * NODE_TILE, (b + 1) * NODE_TILE)
-            piece, first = divmod(b * NODE_TILE, X_PIECE)
-            in_piece = slice(first, first + NODE_TILE)
-            pre = psum.tile([P, PACK, NODE_TILE], F32, name="pre", tag="pre%d" % (b % PRE_BANKS))
+            bank = psum.tile([P, PACK, NODE_TILE], F32, name="pre", tag="pre%d" % (b % PRE_BANKS))
             for j in range(PACK):
                 cols = slice(j * P, (j + 1) * P)
                 nc.tensor.matmul_mx(
-                    out=pre[:, j, :],
+                    out=bank[:, j, :],
                     lhsT=w2_codes[:, cols].bitcast(FP8X4),
                     lhsT_scale=w2_scales[:, cols],
                     rhs=ew[:, nodes].bitcast(FP8X4),
                     rhs_scale=es[E_ROW:P, nodes],
-                    start=True,
+                    start=(j == 0),
                     stop=False,
                 )
+            pre.append(bank)
+
+        for b in range(PRE_BANKS):
+            passes_over_e(b)
+
+        tile_cols = NODE_TILE // LIST_ROWS
+        xw = []
+        for u, count in enumerate(X_PIECES):
+            first = len(xw)
+            piece = gather_words(
+                own("xw%d" % u, [P, count * NODE_TILE], U32),
+                xw_tab,
+                offs_t[:, first * tile_cols : (first + count) * tile_cols],
+            )
+            xw.extend([piece[:, c * NODE_TILE : (c + 1) * NODE_TILE] for c in range(count)])
+        vw = gather_words(own("vw", [P, V], U32), vw_tab, cand_t[:])
+
+        h_bf = []
+        for b in tiles:
+            if b >= PRE_BANKS:
+                passes_over_e(b)
+            nodes = slice(b * NODE_TILE, (b + 1) * NODE_TILE)
+            for j in range(PACK):
                 nc.tensor.matmul_mx(
-                    out=pre[:, j, :],
-                    lhsT=w1_codes[:, cols].bitcast(FP8X4),
-                    lhsT_scale=w1_scales[:, cols],
-                    rhs=xw[piece][:, in_piece].bitcast(FP8X4),
-                    rhs_scale=xs[X_ROW:P, nodes],
+                    out=pre[b][:, j, :],
+                    lhsT=w1_codes[j].bitcast(FP8X4),
+                    lhsT_scale=w1_scales[j],
+                    rhs=xw[b].bitcast(FP8X4),
+                    rhs_scale=xs[:, nodes],
                     start=False,
-                    stop=True,
+                    stop=(j == PACK - 1),
                 )
             hb = own("h_bf%d" % b, [P, NODE_TILE, PACK], BF16)
-            nc.scalar.activation(hb[:], pre[:].rearrange("p j n -> p n j"), ACT.Silu)
+            nc.scalar.activation(hb[:], pre[b][:].rearrange("p j n -> p n j"), ACT.Silu)
             h_bf.append(hb)
 
         logits = []
@@ -176,7 +203,7 @@ def tile_picked_zfrs_silu_p_kernel(
                 lhsT=h_codes[:].bitcast(FP8X4),
                 lhsT_scale=h_scales[:],
                 rhs=vw[:].bitcast(FP8X4),
-                rhs_scale=vs[V_ROW:P, :],
+                rhs_scale=vs[:],
                 start=True,
                 stop=True,
             )

@@ -27,9 +27,9 @@ X_PIECES = (1, 1, 2)
 E_ROW = 4
 PRE_BANKS = 3
 TABLE_STEP = P // BLOCKS
-W2_ON_SCALAR, W1_ON_SCALAR = 128, 50
+W2_ON_SCALAR, W1_ON_SCALAR = 128, 40
 V_WORDS_AT = 0
-MAXIMA_AT = V_WORDS_AT + 4 * G
+MAXIMA_AT = V_WORDS_AT + V
 
 
 def tile_picked_zfrs_silu_p_kernel(
@@ -124,8 +124,8 @@ def tile_picked_zfrs_silu_p_kernel(
         xw_tab = load_words(own("xw_tab", [P, T], I32), x_words)
         xs_picked = gather_scales(own("xs_picked", [P, S], U8), xs_tab, offs_t)
         place_scales(xs, xs_picked)
-        vw_tab = load_words(placed("vw_tab", [P, G], I32, V_WORDS_AT), v_words)
-        vs_picked = gather_scales(own("vs_picked", [P, V], U8), vs_tab, cand_t)
+        vw_tab = load_words(own("vw_tab", [P, G], I32), v_words)
+        vs_picked = gather_scales(placed("vs_picked", [P, V], U8, V_WORDS_AT), vs_tab, cand_t)
         place_scales(vs, vs_picked)
 
         w2_bf = cast(own("w2_bf", [P, H * PACK], BF16), w2_raw, W2_ON_SCALAR, slice(0, PACK))

@@ -71,9 +71,9 @@ def tile_picked_zfrs_silu_p_kernel(
             nc.vector.memset(plane[:].bitcast(I32), 0)
             return plane
 
-        def place_scales(plane, picked):
-            for r in range(PACK):
-                nc.sync.dma_start(
+        def place_scales(plane, picked, queues):
+            for r, queue in enumerate(queues):
+                queue.dma_start(
                     plane[r:P:QUADRANT, :].bitcast(I32),
                     picked[r * TABLE_STEP : P : QUADRANT, :].bitcast(I32),
                 )
@@ -123,10 +123,10 @@ def tile_picked_zfrs_silu_p_kernel(
         es = gather_scales(own("es", [P, S], U8), es_tab, tok_t)
         xw_tab = load_words(own("xw_tab", [P, T], I32), x_words)
         xs_picked = gather_scales(own("xs_picked", [P, S], U8), xs_tab, offs_t)
-        place_scales(xs, xs_picked)
+        place_scales(xs, xs_picked, [nc.sync] * PACK)
         vw_tab = load_words(own("vw_tab", [P, G], I32), v_words)
         vs_picked = gather_scales(placed("vs_picked", [P, V], U8, V_WORDS_AT), vs_tab, cand_t)
-        place_scales(vs, vs_picked)
+        place_scales(vs, vs_picked, [nc.gpsimd, nc.gpsimd, nc.sync, nc.sync])
 
         w2_bf = cast(own("w2_bf", [P, H * PACK], BF16), w2_raw, W2_ON_SCALAR, slice(0, PACK))
         w2_scales = own("w2_scales", [P, H], U8)

@@ -25,7 +25,7 @@ ALIGN = 64
 NODE_TILE = 128
 X_PIECES = (1, 1, 2)
 E_ROW = 4
-PRE_BANKS = 3
+EARLY_TILES = 3
 TABLE_STEP = P // BLOCKS
 W2_ON_SCALAR, W1_ON_SCALAR = 128, 40
 V_WORDS_AT = 0
@@ -141,25 +141,23 @@ def tile_picked_zfrs_silu_p_kernel(
             w1_codes.extend([codes[:, 0:P], codes[:, P : 2 * P]])
 
         tiles = range(S // NODE_TILE)
-        pre = []
+        pre = [psum.tile([P, PACK, NODE_TILE], F32, name="pre%d" % b) for b in tiles]
 
         def passes_over_e(b):
             nodes = slice(b * NODE_TILE, (b + 1) * NODE_TILE)
-            bank = psum.tile([P, PACK, NODE_TILE], F32, name="pre", tag="pre%d" % (b % PRE_BANKS))
             for j in range(PACK):
                 cols = slice(j * P, (j + 1) * P)
                 nc.tensor.matmul_mx(
-                    out=bank[:, j, :],
+                    out=pre[b][:, j, :],
                     lhsT=w2_codes[:, cols].bitcast(FP8X4),
                     lhsT_scale=w2_scales[:, cols],
                     rhs=ew[:, nodes].bitcast(FP8X4),
                     rhs_scale=es[E_ROW:P, nodes],
-                    start=(j == 0),
-                    stop=False,
+                    start=(j == 0 and b < EARLY_TILES),
+                    stop=(j == PACK - 1 and b >= EARLY_TILES),
                 )
-            pre.append(bank)
 
-        for b in range(PRE_BANKS):
+        for b in range(EARLY_TILES):
             passes_over_e(b)
 
         tile_cols = NODE_TILE // LIST_ROWS
@@ -176,8 +174,6 @@ def tile_picked_zfrs_silu_p_kernel(
 
         h_bf = []
         for b in tiles:
-            if b >= PRE_BANKS:
-                passes_over_e(b)
             nodes = slice(b * NODE_TILE, (b + 1) * NODE_TILE)
             for j in range(PACK):
                 nc.tensor.matmul_mx(
@@ -186,16 +182,21 @@ def tile_picked_zfrs_silu_p_kernel(
                     lhsT_scale=w1_scales[j],
                     rhs=xw[b].bitcast(FP8X4),
                     rhs_scale=xs[:, nodes],
-                    start=False,
-                    stop=(j == PACK - 1),
+                    start=(j == 0 and b >= EARLY_TILES),
+                    stop=(j == PACK - 1 and b < EARLY_TILES),
                 )
+            if b >= EARLY_TILES:
+                passes_over_e(b)
             hb = own("h_bf%d" % b, [P, NODE_TILE, PACK], BF16)
             nc.scalar.activation(hb[:], pre[b][:].rearrange("p j n -> p n j"), ACT.Silu)
             h_bf.append(hb)
 
         logits = []
         for b in tiles:
-            h_scales = placed("h%d_scales" % b, [P, NODE_TILE], U8, V_WORDS_AT + b * NODE_TILE)
+            if b == 0:
+                h_scales = own("h0_scales", [P, NODE_TILE], U8)
+            else:
+                h_scales = placed("h%d_scales" % b, [P, NODE_TILE], U8, V_WORDS_AT + b * NODE_TILE)
             h_codes = quantize("h%d_codes" % b, h_bf[b][:].rearrange("p n j -> p (n j)"), h_scales)
             y = psum.tile([P, V], F32, name="y%d" % b)
             nc.tensor.matmul_mx(

@@ -22,14 +22,15 @@ QUADRANT = 32
 BLOCKS = K // 32
 LIST_ROWS = 16
 ALIGN = 64
+BANK = 2048
 NODE_TILE = 128
 X_PIECES = (1, 1, 2)
-E_ROW = 4
-EARLY_TILES = 3
 TABLE_STEP = P // BLOCKS
+E_ROW, X_ROW, V_ROW = 4, 0, 0
 W2_ON_SCALAR, W1_ON_SCALAR = 128, 40
-V_WORDS_AT = 0
-MAXIMA_AT = V_WORDS_AT + V
+EARLY_TILES = 3
+V_PICKED_AT = 0
+MAXIMA_AT = V_PICKED_AT + V
 
 
 def tile_picked_zfrs_silu_p_kernel(
@@ -47,14 +48,17 @@ def tile_picked_zfrs_silu_p_kernel(
         def placed(name, shape, dtype, offset):
             return shared.tile(shape, dtype, name=name, align_bytes=ALIGN, offset=offset)
 
+        def bank(name, shape, number):
+            return psum.tile(shape, F32, name=name, offset=number * BANK)
+
         def load_list(name, src):
             lst = keep.tile([P, S // LIST_ROWS], U16, name=name)
             nc.sync.dma_start(lst[:], src)
             return lst
 
-        def load_scales(table, src, queue):
+        def load_scales(table, src, first):
             nc.vector.memset(table[:].bitcast(I32), 0)
-            queue.dma_start(table[0:P:TABLE_STEP, :].bitcast(I32), src[0].bitcast(I32))
+            nc.sync.dma_start(table[first:P:TABLE_STEP, :].bitcast(I32), src[0].bitcast(I32))
             return table
 
         def load_plane(table, src, row):
@@ -71,11 +75,11 @@ def tile_picked_zfrs_silu_p_kernel(
             nc.vector.memset(plane[:].bitcast(I32), 0)
             return plane
 
-        def place_scales(plane, picked, queues):
+        def place_scales(plane, row, picked, first, queues):
             for r, queue in enumerate(queues):
                 queue.dma_start(
-                    plane[r:P:QUADRANT, :].bitcast(I32),
-                    picked[r * TABLE_STEP : P : QUADRANT, :].bitcast(I32),
+                    plane[row + r : P : QUADRANT, :].bitcast(I32),
+                    picked[first + r * TABLE_STEP : P : QUADRANT, :].bitcast(I32),
                 )
             return plane
 
@@ -110,27 +114,29 @@ def tile_picked_zfrs_silu_p_kernel(
 
         ew_tab = load_words(own("ew_tab", [P, W], I32), e_words)
         tok_t = load_list("tok_t", tok)
-        es_tab = load_plane(own("es_tab", [P, W], U8), e_scales, E_ROW)
         offs_t = load_list("offs_t", offs)
+        xs_tab = load_scales(own("xs_tab", [P, T], U8), x_scales, 0)
         w2_raw = load_weight(own("w2_raw", [P, PACK, H], F32), w2)
-        xs_tab = load_scales(own("xs_tab", [P, T], U8), x_scales, nc.sync)
         cand_t = load_list("cand_t", cand)
-        vs_tab = load_scales(own("vs_tab", [P, G], U8), v_scales, nc.sync)
+        vs_tab = load_scales(own("vs_tab", [P, G], U8), v_scales, 0)
+        es_tab = load_plane(own("es_tab", [P, W], U8), e_scales, E_ROW)
         w1_raw = load_weight(own("w1_raw", [P, PACK, H], F32), w1)
         xs, vs = [cleared_plane(name) for name in ("xs", "vs")]
 
         ew = gather_words(own("ew", [P, S], U32), ew_tab, tok_t[:])
-        es = gather_scales(own("es", [P, S], U8), es_tab, tok_t)
         xw_tab = load_words(own("xw_tab", [P, T], I32), x_words)
         xs_picked = gather_scales(own("xs_picked", [P, S], U8), xs_tab, offs_t)
-        place_scales(xs, xs_picked, [nc.sync] * PACK)
+        place_scales(xs, X_ROW, xs_picked, 0, [nc.sync] * PACK)
         vw_tab = load_words(own("vw_tab", [P, G], I32), v_words)
-        vs_picked = gather_scales(placed("vs_picked", [P, V], U8, V_WORDS_AT), vs_tab, cand_t)
-        place_scales(vs, vs_picked, [nc.gpsimd, nc.gpsimd, nc.sync, nc.sync])
+        vs_picked = gather_scales(placed("vs_picked", [P, V], U8, V_PICKED_AT), vs_tab, cand_t)
+        place_scales(vs, V_ROW, vs_picked, 0, [nc.gpsimd, nc.gpsimd, nc.sync, nc.sync])
+        es = gather_scales(own("es", [P, S], U8), es_tab, tok_t)
 
         w2_bf = cast(own("w2_bf", [P, H * PACK], BF16), w2_raw, W2_ON_SCALAR, slice(0, PACK))
         w2_scales = own("w2_scales", [P, H], U8)
         w2_codes = quantize("w2_codes", w2_bf[:], w2_scales)
+
+
         w1_codes, w1_scales = [], []
         halves = [cast(own("w1_bf%d" % u, [P, H * PACK // 2], BF16), w1_raw, share, slice(2 * u, 2 * u + 2))
                   for u, share in enumerate((P, W1_ON_SCALAR))]
@@ -141,24 +147,45 @@ def tile_picked_zfrs_silu_p_kernel(
             w1_codes.extend([codes[:, 0:P], codes[:, P : 2 * P]])
 
         tiles = range(S // NODE_TILE)
-        pre = [psum.tile([P, PACK, NODE_TILE], F32, name="pre%d" % b) for b in tiles]
+        per_bank = [PACK] * len(tiles)
+        pre = [bank("pre%d" % b, [P, PACK, NODE_TILE], b) for b in tiles]
+        sums = [[pre[b][:, j, :] for j in range(PACK)] for b in tiles]
+        logit_banks = [4, 5, 6, 7]
 
-        def passes_over_e(b):
+        def e_pass(b, j, start, stop):
             nodes = slice(b * NODE_TILE, (b + 1) * NODE_TILE)
-            for j in range(PACK):
-                cols = slice(j * P, (j + 1) * P)
-                nc.tensor.matmul_mx(
-                    out=pre[b][:, j, :],
-                    lhsT=w2_codes[:, cols].bitcast(FP8X4),
-                    lhsT_scale=w2_scales[:, cols],
-                    rhs=ew[:, nodes].bitcast(FP8X4),
-                    rhs_scale=es[E_ROW:P, nodes],
-                    start=(j == 0 and b < EARLY_TILES),
-                    stop=(j == PACK - 1 and b >= EARLY_TILES),
-                )
+            cols = slice(j * P, (j + 1) * P)
+            nc.tensor.matmul_mx(
+                out=sums[b][j],
+                lhsT=w2_codes[:, cols].bitcast(FP8X4),
+                lhsT_scale=w2_scales[:, cols],
+                rhs=ew[:, nodes].bitcast(FP8X4),
+                rhs_scale=es[E_ROW:P, nodes],
+                start=start,
+                stop=stop,
+            )
+
+        def x_pass(b, j, start, stop):
+            nodes = slice(b * NODE_TILE, (b + 1) * NODE_TILE)
+            nc.tensor.matmul_mx(
+                out=sums[b][j],
+                lhsT=w1_codes[j].bitcast(FP8X4),
+                lhsT_scale=w1_scales[j],
+                rhs=xw[b].bitcast(FP8X4),
+                rhs_scale=xs[X_ROW:P, nodes],
+                start=start,
+                stop=stop,
+            )
+
+        def opens(b, j):
+            return j % per_bank[b] == 0
+
+        def closes(b, j):
+            return j % per_bank[b] == per_bank[b] - 1
 
         for b in range(EARLY_TILES):
-            passes_over_e(b)
+            for j in range(PACK):
+                e_pass(b, j, opens(b, j), False)
 
         tile_cols = NODE_TILE // LIST_ROWS
         xw = []
@@ -170,23 +197,17 @@ def tile_picked_zfrs_silu_p_kernel(
                 offs_t[:, first * tile_cols : (first + count) * tile_cols],
             )
             xw.extend([piece[:, c * NODE_TILE : (c + 1) * NODE_TILE] for c in range(count)])
+
         vw = gather_words(own("vw", [P, V], U32), vw_tab, cand_t[:])
 
         h_bf = []
         for b in tiles:
-            nodes = slice(b * NODE_TILE, (b + 1) * NODE_TILE)
+            early = b < EARLY_TILES
             for j in range(PACK):
-                nc.tensor.matmul_mx(
-                    out=pre[b][:, j, :],
-                    lhsT=w1_codes[j].bitcast(FP8X4),
-                    lhsT_scale=w1_scales[j],
-                    rhs=xw[b].bitcast(FP8X4),
-                    rhs_scale=xs[:, nodes],
-                    start=(j == 0 and b >= EARLY_TILES),
-                    stop=(j == PACK - 1 and b < EARLY_TILES),
-                )
-            if b >= EARLY_TILES:
-                passes_over_e(b)
+                x_pass(b, j, opens(b, j) and not early, closes(b, j) and early)
+            if not early:
+                for j in range(PACK):
+                    e_pass(b, j, False, closes(b, j))
             hb = own("h_bf%d" % b, [P, NODE_TILE, PACK], BF16)
             nc.scalar.activation(hb[:], pre[b][:].rearrange("p j n -> p n j"), ACT.Silu)
             h_bf.append(hb)
@@ -196,15 +217,15 @@ def tile_picked_zfrs_silu_p_kernel(
             if b == 0:
                 h_scales = own("h0_scales", [P, NODE_TILE], U8)
             else:
-                h_scales = placed("h%d_scales" % b, [P, NODE_TILE], U8, V_WORDS_AT + b * NODE_TILE)
+                h_scales = placed("h%d_scales" % b, [P, NODE_TILE], U8, V_PICKED_AT + b * NODE_TILE)
             h_codes = quantize("h%d_codes" % b, h_bf[b][:].rearrange("p n j -> p (n j)"), h_scales)
-            y = psum.tile([P, V], F32, name="y%d" % b)
+            y = bank("y%d" % b, [P, V], logit_banks[b])
             nc.tensor.matmul_mx(
                 out=y[:],
                 lhsT=h_codes[:].bitcast(FP8X4),
                 lhsT_scale=h_scales[:],
                 rhs=vw[:].bitcast(FP8X4),
-                rhs_scale=vs[:],
+                rhs_scale=vs[V_ROW:P, :],
                 start=True,
                 stop=True,
             )

@@ -30,7 +30,7 @@ E_ROW, X_ROW, V_ROW = 4, 0, 0
 W2_ON_SCALAR, W1_ON_SCALAR = 128, 40
 EARLY_TILES = 3
 V_PICKED_AT = 0
-MAXIMA_AT = V_PICKED_AT + V
+MAXIMA_AT = V_PICKED_AT + S + V
 
 
 def tile_picked_zfrs_silu_p_kernel(
@@ -121,15 +121,27 @@ def tile_picked_zfrs_silu_p_kernel(
         vs_tab = load_scales(own("vs_tab", [P, G], U8), v_scales, 0)
         es_tab = load_plane(own("es_tab", [P, W], U8), e_scales, E_ROW)
         w1_raw = load_weight(own("w1_raw", [P, PACK, H], F32), w1)
-        xs, vs = [cleared_plane(name) for name in ("xs", "vs")]
+        planes = own("planes", [P, S + V], U8)
+        nc.vector.memset(planes[:].bitcast(I32), 0)
+        picked = placed("picked", [P, S + V], U8, V_PICKED_AT)
+        x_cols, v_cols, both = slice(0, S), slice(S, S + V), slice(0, S + V)
+        xs, vs = planes[:, x_cols], planes[:, v_cols]
+
+        def place_row(r, cols):
+            nc.sync.dma_start(
+                planes[r:P:QUADRANT, cols].bitcast(I32),
+                picked[r * TABLE_STEP : P : QUADRANT, cols].bitcast(I32),
+            )
 
         ew = gather_words(own("ew", [P, S], U32), ew_tab, tok_t[:])
         xw_tab = load_words(own("xw_tab", [P, T], I32), x_words)
-        xs_picked = gather_scales(own("xs_picked", [P, S], U8), xs_tab, offs_t)
-        place_scales(xs, X_ROW, xs_picked, 0, [nc.sync] * PACK)
+        nc.vector.tensor_copy(picked[:, x_cols], xs_tab[:].indirect(offs_t[:]))
+        nc.vector.tensor_copy(picked[:, v_cols], vs_tab[:].indirect(cand_t[:]))
+        for r, cols in enumerate((x_cols, x_cols, both, both)):
+            place_row(r, cols)
         vw_tab = load_words(own("vw_tab", [P, G], I32), v_words)
-        vs_picked = gather_scales(placed("vs_picked", [P, V], U8, V_PICKED_AT), vs_tab, cand_t)
-        place_scales(vs, V_ROW, vs_picked, 0, [nc.gpsimd, nc.gpsimd, nc.sync, nc.sync])
+        for r in range(2):
+            place_row(r, v_cols)
         es = gather_scales(own("es", [P, S], U8), es_tab, tok_t)
 
         w2_bf = cast(own("w2_bf", [P, H * PACK], BF16), w2_raw, W2_ON_SCALAR, slice(0, PACK))
@@ -172,7 +184,7 @@ def tile_picked_zfrs_silu_p_kernel(
                 lhsT=w1_codes[j].bitcast(FP8X4),
                 lhsT_scale=w1_scales[j],
                 rhs=xw[b].bitcast(FP8X4),
-                rhs_scale=xs[X_ROW:P, nodes],
+                rhs_scale=xs[:, nodes],
                 start=start,
                 stop=stop,
             )
@@ -225,7 +237,7 @@ def tile_picked_zfrs_silu_p_kernel(
                 lhsT=h_codes[:].bitcast(FP8X4),
                 lhsT_scale=h_scales[:],
                 rhs=vw[:].bitcast(FP8X4),
-                rhs_scale=vs[V_ROW:P, :],
+                rhs_scale=vs,
                 start=True,
                 stop=True,
             )

@@ -226,10 +226,7 @@ def tile_picked_zfrs_silu_p_kernel(
 
         logits = []
         for b in tiles:
-            if b == 0:
-                h_scales = own("h0_scales", [P, NODE_TILE], U8)
-            else:
-                h_scales = placed("h%d_scales" % b, [P, NODE_TILE], U8, V_PICKED_AT + b * NODE_TILE)
+            h_scales = placed("h%d_scales" % b, [P, NODE_TILE], U8, V_PICKED_AT + b * NODE_TILE)
             h_codes = quantize("h%d_codes" % b, h_bf[b][:].rearrange("p n j -> p (n j)"), h_scales)
             y = bank("y%d" % b, [P, V], logit_banks[b])
             nc.tensor.matmul_mx(

@@ -29,6 +29,7 @@ TABLE_STEP = P // BLOCKS
 E_ROW, X_ROW, V_ROW = 4, 0, 0
 W2_ON_SCALAR, W1_ON_SCALAR = 128, 40
 EARLY_TILES = 3
+XV_ROW = 12
 V_PICKED_AT = 0
 MAXIMA_AT = V_PICKED_AT + S + V
 
@@ -125,11 +126,11 @@ def tile_picked_zfrs_silu_p_kernel(
         nc.vector.memset(planes[:].bitcast(I32), 0)
         picked = placed("picked", [P, S + V], U8, V_PICKED_AT)
         x_cols, v_cols, both = slice(0, S), slice(S, S + V), slice(0, S + V)
-        xs, vs = planes[:, x_cols], planes[:, v_cols]
+        xs, vs = planes[XV_ROW:P, x_cols], planes[XV_ROW:P, v_cols]
 
         def place_row(r, cols):
             nc.sync.dma_start(
-                planes[r:P:QUADRANT, cols].bitcast(I32),
+                planes[XV_ROW + r : P : QUADRANT, cols].bitcast(I32),
                 picked[r * TABLE_STEP : P : QUADRANT, cols].bitcast(I32),
             )
 

from contextlib import ExitStack

import concourse.mybir as mybir

K, T, S, W, V, H, G = 512, 2048, 512, 1024, 512, 512, 2048
FLOPS = 2 * (2 * K * H * S + H * S * V)

F32 = mybir.dt.float32
BF16 = mybir.dt.bfloat16
I32 = mybir.dt.int32
U32 = mybir.dt.uint32
U16 = mybir.dt.uint16
U8 = mybir.dt.uint8
FP8X4 = mybir.dt.float8_e4m3fn_x4
ACT = mybir.ActivationFunctionType
ALU = mybir.AluOpType
AX = mybir.AxisListType

P = 128
PACK = 4
QUADRANT = 32
BLOCKS = K // 32
LIST_ROWS = 16
ALIGN = 64
BANK = 2048
NODE_TILE = 128
X_PIECES = (1, 1, 2)
TABLE_STEP = P // BLOCKS
E_ROW, X_ROW, V_ROW = 4, 0, 0
W2_ON_SCALAR, W1_ON_SCALAR = 128, 40
EARLY_TILES = 3
XV_ROW = 12
V_PICKED_AT = 0
MAXIMA_AT = V_PICKED_AT + S + V


def tile_picked_zfrs_silu_p_kernel(
    tc, x_words, x_scales, e_words, e_scales, w1, w2, v_words, v_scales, offs, tok, cand, out
):
    nc = tc.nc
    with ExitStack() as ctx:
        keep = ctx.enter_context(tc.tile_pool(name="keep", bufs=1))
        shared = ctx.enter_context(tc.tile_pool(name="shared", bufs=1))
        psum = ctx.enter_context(tc.psum_pool(name="psum", bufs=1))

        def own(name, shape, dtype):
            return keep.tile(shape, dtype, name=name, align_bytes=ALIGN)

        def placed(name, shape, dtype, offset):
            return shared.tile(shape, dtype, name=name, align_bytes=ALIGN, offset=offset)

        def bank(name, shape, number):
            return psum.tile(shape, F32, name=name, offset=number * BANK)

        def load_list(name, src):
            lst = keep.tile([P, S // LIST_ROWS], U16, name=name)
            nc.sync.dma_start(lst[:], src)
            return lst

        def load_scales(table, src, first):
            nc.vector.memset(table[:].bitcast(I32), 0)
            nc.sync.dma_start(table[first:P:TABLE_STEP, :].bitcast(I32), src[0].bitcast(I32))
            return table

        def load_plane(table, src, row):
            nc.vector.memset(table[:].bitcast(I32), 0)
            for r in range(PACK):
                nc.sync.dma_start(
                    table[row + r : P : QUADRANT, :].bitcast(I32),
                    src[0, r:BLOCKS:PACK, :].bitcast(I32),
                )
            return table

        def cleared_plane(name):
            plane = own(name, [P, S], U8)
            nc.vector.memset(plane[:].bitcast(I32), 0)
            return plane

        def place_scales(plane, row, picked, first, queues):
            for r, queue in enumerate(queues):
                queue.dma_start(
                    plane[row + r : P : QUADRANT, :].bitcast(I32),
                    picked[first + r * TABLE_STEP : P : QUADRANT, :].bitcast(I32),
                )
            return plane

        def load_words(table, src):
            nc.sync.dma_start(table[:], src[0].rearrange("p n r -> p (n r)").bitcast(I32))
            return table

        def load_weight(raw, src):
            nc.sync.dma_start(raw[:], src.rearrange("(p r) c -> p r c", r=PACK))
            return raw

        def gather_scales(picked, table, lst):
            nc.vector.tensor_copy(picked[:], table[:].indirect(lst[:]))
            return picked

        def gather_words(picked, table, entries):
            nc.vector.tensor_copy(picked[:], table[:].bitcast(U32).indirect(entries))
            return picked

        def cast(grouped, raw, on_scalar, js):
            dst = grouped[:].rearrange("p (j m r) -> p m r j", m=P, r=PACK)
            src = raw[:].rearrange("p r (m j) -> p m r j", j=PACK)[:, :, :, js]
            nc.scalar.copy(dst[:, :on_scalar], src[:, :on_scalar])
            if on_scalar < P:
                nc.vector.tensor_copy(dst[:, on_scalar:], src[:, on_scalar:])
            return grouped

        def quantize(name, src, scales):
            codes = own(name, scales.shape, U32)
            nc.vector.quantize_mx(out=codes[:].bitcast(FP8X4), scales=scales[:], in_=src)
            return codes

        ew_tab = load_words(own("ew_tab", [P, W], I32), e_words)
        tok_t = load_list("tok_t", tok)
        offs_t = load_list("offs_t", offs)
        xs_tab = load_scales(own("xs_tab", [P, T], U8), x_scales, 0)
        w2_raw = load_weight(own("w2_raw", [P, PACK, H], F32), w2)
        cand_t = load_list("cand_t", cand)
        vs_tab = load_scales(own("vs_tab", [P, G], U8), v_scales, 0)
        es_tab = load_plane(own("es_tab", [P, W], U8), e_scales, E_ROW)
        w1_raw = load_weight(own("w1_raw", [P, PACK, H], F32), w1)
        planes = own("planes", [P, S + V], U8)
        nc.vector.memset(planes[:].bitcast(I32), 0)
        picked = placed("picked", [P, S + V], U8, V_PICKED_AT)
        x_cols, v_cols, both = slice(0, S), slice(S, S + V), slice(0, S + V)
        xs, vs = planes[XV_ROW:P, x_cols], planes[XV_ROW:P, v_cols]

        def place_row(r, cols):
            nc.sync.dma_start(
                planes[XV_ROW + r : P : QUADRANT, cols].bitcast(I32),
                picked[r * TABLE_STEP : P : QUADRANT, cols].bitcast(I32),
            )

        ew = gather_words(own("ew", [P, S], U32), ew_tab, tok_t[:])
        xw_tab = load_words(own("xw_tab", [P, T], I32), x_words)
        nc.vector.tensor_copy(picked[:, x_cols], xs_tab[:].indirect(offs_t[:]))
        nc.vector.tensor_copy(picked[:, v_cols], vs_tab[:].indirect(cand_t[:]))
        for r, cols in enumerate((x_cols, x_cols, both, both)):
            place_row(r, cols)
        vw_tab = load_words(own("vw_tab", [P, G], I32), v_words)
        for r in range(2):
            place_row(r, v_cols)
        es = gather_scales(own("es", [P, S], U8), es_tab, tok_t)

        w2_bf = cast(own("w2_bf", [P, H * PACK], BF16), w2_raw, W2_ON_SCALAR, slice(0, PACK))
        w2_scales = own("w2_scales", [P, H], U8)
        w2_codes = quantize("w2_codes", w2_bf[:], w2_scales)


        w1_codes, w1_scales = [], []
        halves = [cast(own("w1_bf%d" % u, [P, H * PACK // 2], BF16), w1_raw, share, slice(2 * u, 2 * u + 2))
                  for u, share in enumerate((P, W1_ON_SCALAR))]
        for u, half in enumerate(halves):
            scales = own("w1_scales%d" % u, [P, H // 2], U8)
            codes = quantize("w1_codes%d" % u, half[:], scales)
            w1_scales.extend([scales[:, 0:P], scales[:, P : 2 * P]])
            w1_codes.extend([codes[:, 0:P], codes[:, P : 2 * P]])

        tiles = range(S // NODE_TILE)
        per_bank = [PACK] * len(tiles)
        pre = [bank("pre%d" % b, [P, PACK, NODE_TILE], b) for b in tiles]
        sums = [[pre[b][:, j, :] for j in range(PACK)] for b in tiles]
        logit_banks = [4, 5, 6, 7]

        def e_pass(b, j, start, stop):
            nodes = slice(b * NODE_TILE, (b + 1) * NODE_TILE)
            cols = slice(j * P, (j + 1) * P)
            nc.tensor.matmul_mx(
                out=sums[b][j],
                lhsT=w2_codes[:, cols].bitcast(FP8X4),
                lhsT_scale=w2_scales[:, cols],
                rhs=ew[:, nodes].bitcast(FP8X4),
                rhs_scale=es[E_ROW:P, nodes],
                start=start,
                stop=stop,
            )

        def x_pass(b, j, start, stop):
            nodes = slice(b * NODE_TILE, (b + 1) * NODE_TILE)
            nc.tensor.matmul_mx(
                out=sums[b][j],
                lhsT=w1_codes[j].bitcast(FP8X4),
                lhsT_scale=w1_scales[j],
                rhs=xw[b].bitcast(FP8X4),
                rhs_scale=xs[:, nodes],
                start=start,
                stop=stop,
            )

        def opens(b, j):
            return j % per_bank[b] == 0

        def closes(b, j):
            return j % per_bank[b] == per_bank[b] - 1

        for b in range(EARLY_TILES):
            for j in range(PACK):
                e_pass(b, j, opens(b, j), False)

        tile_cols = NODE_TILE // LIST_ROWS
        xw = []
        for u, count in enumerate(X_PIECES):
            first = len(xw)
            piece = gather_words(
                own("xw%d" % u, [P, count * NODE_TILE], U32),
                xw_tab,
                offs_t[:, first * tile_cols : (first + count) * tile_cols],
            )
            xw.extend([piece[:, c * NODE_TILE : (c + 1) * NODE_TILE] for c in range(count)])

        vw = gather_words(own("vw", [P, V], U32), vw_tab, cand_t[:])

        h_bf = []
        for b in tiles:
            early = b < EARLY_TILES
            for j in range(PACK):
                x_pass(b, j, opens(b, j) and not early, closes(b, j) and early)
            if not early:
                for j in range(PACK):
                    e_pass(b, j, False, closes(b, j))
            hb = own("h_bf%d" % b, [P, NODE_TILE, PACK], BF16)
            nc.scalar.activation(hb[:], pre[b][:].rearrange("p j n -> p n j"), ACT.Silu)
            h_bf.append(hb)

        logits = []
        for b in tiles:
            h_scales = placed("h%d_scales" % b, [P, NODE_TILE], U8, V_PICKED_AT + b * NODE_TILE)
            h_codes = quantize("h%d_codes" % b, h_bf[b][:].rearrange("p n j -> p (n j)"), h_scales)
            y = bank("y%d" % b, [P, V], logit_banks[b])
            nc.tensor.matmul_mx(
                out=y[:],
                lhsT=h_codes[:].bitcast(FP8X4),
                lhsT_scale=h_scales[:],
                rhs=vw[:].bitcast(FP8X4),
                rhs_scale=vs,
                start=True,
                stop=True,
            )
            logits.append(y)

        def max_at(b):
            return MAXIMA_AT + b * ALIGN

        def negated_max(b, offset):
            neg = placed("neg_max%d" % b, [P, 1], F32, offset)
            nc.vector.tensor_reduce(neg[:], logits[b][:], AX.X, ALU.max, negate=True)
            return neg

        def exp_and_inverse_sum(b):
            ex = own("ex%d" % b, [P, V], F32)
            total = own("total%d" % b, [P, 1], F32)
            nc.scalar.activation(
                ex[:], logits[b][:], ACT.Exp, bias=neg_max[b][:], accum_out=total[:]
            )
            inv = own("inv%d" % b, [P, 1], F32)
            nc.vector.reciprocal(inv[:], total[:])
            return ex, inv

        def scale_and_store(b, res, ex, inv):
            nc.vector.tensor_scalar(res[:], ex[:], inv[:], None, ALU.mult)
            nc.sync.dma_start(out[b * NODE_TILE : (b + 1) * NODE_TILE, :], res[:])

        neg_max = [negated_max(b, max_at(b)) for b in range(3)]
        parts_0 = exp_and_inverse_sum(0)
        neg_max.append(negated_max(3, max_at(0)))
        scale_and_store(0, own("res0", [P, V], F32), *parts_0)
        parts_1 = exp_and_inverse_sum(1)
        parts_2 = exp_and_inverse_sum(2)
        scale_and_store(1, placed("res1", [P, V], F32, max_at(2)), *parts_1)
        scale_and_store(2, own("res2", [P, V], F32), *parts_2)
        scale_and_store(3, own("res3", [P, V], F32), *exp_and_inverse_sum(3))
